import numpy as np, ml_dtypes
CORES = [6,15,38,47]
N = 4
BF = ml_dtypes.bfloat16
W, I, D, T = 4096, 256, 4, 6
B = W // I
def basic(rng):
    return (rng.integers(0, 256, (N, 8, 16, W)), rng.integers(0, W, (N, 8, 16, I)), rng.integers(0, D, (N, 8, 16, I)), rng.integers(0, W, (N, 8, 16, I, D)),
            rng.integers(0, 16, (N, 8, 16)), rng.integers(800, 1151, (N, 8, 16)))
def some(rng, a):
    return np.argsort(rng.random((N, 8, 16, I)), axis=2) < a[:, :, None, :]
def seat(rng, on):
    place = np.argsort(rng.random((N, 8, 16, I)), axis=2)
    near = place + rng.integers(0, 225, (N, 8, 1, I)); far = 15 * place + rng.integers(0, 15, (N, 8, 16, I))
    return np.where(on, np.where(rng.random((N, 8, 1, I)) < 0.5, near, far), -1)
def blame(rng, on, free_, dead):
    o = on.astype(np.int64); order = np.argsort(np.where(on, 0.0, 2.0) + rng.random(on.shape), axis=2); loc = np.argsort(order, axis=2)[..., None]
    cnt = (np.add.reduce(o, axis=2)[:, :, None, :] - o)[..., None]
    m = (rng.random((N, 8, 16, I, D)) * cnt).astype(np.int64); m = np.where(on[..., None] & (m >= loc), m + 1, m)
    who = np.take_along_axis(order[..., None], np.minimum(m, 15), axis=2); who = np.where(cnt > 0, who, -1)
    u = rng.random((N, 8, 16, I, D))
    return np.where(u < free_, -1, np.where(u < free_ + dead, -2, who))
def pack(x, n, q, v, e, c, w, t):
    return {"xt": x.reshape(N, 128, W).astype(BF), "nm": n.reshape(N, 128, I).astype(np.int32), "ps": q.reshape(N, 128, I).astype(BF), "dv": v.reshape(N, 128, I).astype(BF),
            "ex": e.reshape(N, 128, I * D).astype(BF), "dn": c.reshape(N, 128, I * D).astype(np.int32), "wt": w.reshape(N, 128, 1).astype(np.int32), "th": t.reshape(N, 128, 1).astype(np.int32)}
def setup_inputs(rng):
    x, n, v, c, w, t = basic(rng); on = some(rng, rng.integers(0, 17, (N, 8, I)))
    return pack(x, n, seat(rng, on), v, blame(rng, on, rng.choice(np.array([0.03, 0.1, 0.3, 0.7]), (N, 8, 1, I, 1)), 0.1), c, w, t)
def setup_inputs_spread(rng):
    x, n, v, c, w, t = basic(rng)
    x = np.floor(rng.random((N, 8, 16, W)) * np.exp2(rng.integers(0, 9, (N, 8, 1, W)))).astype(np.int64)
    n = (W * rng.random((N, 8, 16, I)) ** 3).astype(np.int64); c = (W * rng.random((N, 8, 16, I, D)) ** 2).astype(np.int64)
    t = np.minimum(np.exp2(12 * rng.random((N, 8, 16))).astype(np.int64) - 1, 4080)
    on = some(rng, (17 * rng.random((N, 8, I)) ** 2).astype(np.int64))
    return pack(x, n, seat(rng, on), v, blame(rng, on, rng.choice(np.array([0.0, 0.2, 0.6]), (N, 8, 1, I, 1)), 0.15), c, w, t)
def setup_inputs_ends(rng):
    x, n, v, c, w, t = basic(rng)
    kind = rng.integers(0, 4, (N, 8, 1, W)); x = np.where(kind == 0, 0, np.where(kind == 1, 255, 255 * rng.integers(0, 2, (N, 8, 16, W))))
    x[..., 0] = 0; x[..., W - 1] = 255; x[..., W - 37] = 0; x[:, ::2, :, W - W // 16 - 38] = 255; x[:, 1::2, :, W - W // 16 - 38] = 0
    x[:, 3, :, W - 37] = np.where(np.argsort(rng.random((N, 16)), axis=1) < 9, 0, 255)
    x[:, 3, :, W - W // 16 - 38] = np.where(np.argsort(rng.random((N, 16)), axis=1) < 11, 0, 255)
    x[:, 5, :, W - 37] = 255
    n = np.where(rng.random(n.shape) < 0.85, (W - 1) * rng.integers(0, 2, n.shape), n); c = np.where(rng.random(c.shape) < 0.85, (W - 1) * rng.integers(0, 2, c.shape), c)
    v = (D - 1) * rng.integers(0, 2, v.shape); w = 15 * rng.integers(0, 2, w.shape); w[:, 7] = 15; w[:, 0, 0] = 0
    z = np.array([0, 4080, 4079, 1])
    t[:, ::2] = rng.choice(z, (N, 4, 16), p=[0.85, 0.05, 0.05, 0.05]); t[:, 1::2] = rng.choice(z, (N, 4, 16), p=[0.3, 0.5, 0.1, 0.1])
    t[:, 7] = 4079; t[:, 7, 5] = 4080; t[:, 7, 14] = 4080; t[:, 5] = 0; t[:, 3] = rng.choice(np.array([2295, 2804]), (N, 16))
    on = some(rng, rng.choice(np.array([0, 1, 2, 4, 8, 15, 16]), (N, 8, I))); on[:, :, 15] |= rng.random((N, 8, I)) < 0.85
    on[:, 7, :, I - 1] = True; on[:, 7, 15, I - 1] = False
    on[:, 7, :, I - 2] = True
    for k in (5, 14, 15): on[:, 7, k, I - 2] = False
    climb = (0, I // 2, (W - W // 16 - 38) // B, (W - 37) // B, I - 1)
    crest = (1, I // 2 + 1, (W - 37) // B - 1)
    for i in climb + crest: on[:, 5, :, i] = False; on[:, 5, 15, i] = True
    place = np.argsort(rng.random((N, 8, 16, I)), axis=2); q = np.where(on, np.where(place < 8, place, 224 + place), -1)
    kk = np.arange(16).reshape(1, 1, 16, 1, 1); u = rng.random((N, 8, 16, I, D)); b = blame(rng, on, 0.5, 0.0)
    hot = np.where(u < 0.4, 15, np.where(u < 0.75, -2, np.where(u < 0.9, -1, b))); calm = np.where(u < 0.7, -2, np.where(u < 0.85, -1, b))
    e = np.where(on[:, :, 15][:, :, None, :, None] & (kk != 15), hot, calm)
    e[:, 7, 15, I - 1] = -1; c[:, 7, 15, I - 1] = W - 1; n[:, 7, 0:15:2, I - 1] = 0; n[:, 7, 1:15:2, I - 1] = W - 1
    e[:, 7, 5, I - 2] = -1; c[:, 7, 5, I - 2] = 0; n[:, 7, :, I - 2] = W - 1
    for i in climb + crest: q[:, 5, 15, i] = 239; e[:, 5, :, i] = -1; n[:, 5, :, i] = W - 1; c[:, 5, :, i] = W - 1
    for i in crest: c[:, 5, T - 2, i] = 0
    return pack(x, n, q, v, e, c, w, t)
def setup_inputs_corners(rng):
    x, n, v, c, w, t = basic(rng)
    x = 32 * rng.integers(0, 8, (N, 8, 16, W)); t = 32 * rng.integers(26, 36, (N, 8, 16)) - rng.integers(0, 2, (N, 8, 16))
    t = np.where(rng.random(t.shape) < 0.08, rng.choice(np.array([0, 4080]), t.shape), t); w = rng.choice(np.array([0, 1, 15]), w.shape)
    n = np.where(rng.random(n.shape) < 0.05, 0, n); c = np.where(rng.random(c.shape) < 0.05, 0, c)
    a = rng.choice(np.array([0, 1, 2, 15, 16]), (N, 8, I)); a[:, 3] = 16; a[1::2, 3, I - 1] = 15
    on = some(rng, a); q = seat(rng, on)
    full = blame(rng, on, 0.0, 0.0); mix = blame(rng, on, 0.0, 0.6); last = full.copy(); last[..., D - 1] = -1
    kk = np.arange(16).reshape(1, 1, 16, 1, 1); j = np.argmax(q, axis=2)[:, :, None, :, None]; some_on = np.any(on, axis=2)[:, :, None, :, None]
    top = np.where((kk != j) & some_on, j, -2); m = rng.integers(0, 7, (N, 8, 1, I, 1))
    e = np.where(m == 0, -1, np.where(m == 1, -2, np.where(m == 2, full, np.where(m == 3, last, np.where(m == 4, full[..., :1], np.where(m == 5, mix, top))))))
    e = np.where(m >= 0, e, np.zeros((N, 8, 16, I, D), np.int64))
    return pack(x, n, q, v, e, c, w, t)
def setup_inputs_crowd(rng):
    x, n, v, c, w, t = basic(rng)
    on = some(rng, rng.choice(np.array([1, 2, 8, 14, 15]), (N, 8, I))); q = seat(rng, on)
    kk = np.arange(16).reshape(1, 1, 16, 1, 1); j = np.argmax(q, axis=2)[:, :, None, :, None]
    own = blame(rng, on, 0.3, 0.1); other = blame(rng, on, 0.0, 0.2)
    own[:, 5] = -1; own[1::2, 5, :, 0] = -2
    e = np.where(kk == j, own, j); alt = np.where(kk == j, own, other); e[:, 1::2, :, :, D - 1] = alt[:, 1::2, :, :, D - 1]
    p = np.argmax(q < 0, axis=2)
    for r in range(1, N, 2): e[r, 7, p[r, 7, I - 1], I - 1, 0] = -1
    t[:, ::3] = 4080; t[:, 1::3] = 4080; t[:, 1::3, 5] = 0; t[:, 5] = 0
    n[:, 0:2] = n[:, 0:2, :1].copy(); c[:, 2] = c[:, 2, :1, :, :1].copy()
    n[:, 5] = (W // 2) * rng.integers(0, 2, (N, 16, I)); c[:, 5] = np.where(c[:, 5] % (W // 8) == 0, c[:, 5] + 1, c[:, 5])
    return pack(x, n, q, v, e, c, w, t)
def setup_inputs_few(rng):
    x, n, v, c, w, t = basic(rng); on = some(rng, rng.integers(0, 17, (N, 8, I))); chains = []
    for r in range(N):
        for g in rng.permutation(8)[:r % 4]:
            i = (0, I - 1, int(rng.integers(0, I)))[int(rng.integers(0, 3))]; on[r, g, :, i] = True; on[r, g, int(rng.integers(0, 16)), i] = False
            chains.append((r, int(g), i, T if r < 4 else int(rng.integers(1, T + 1))))
    q = seat(rng, on); e = np.where(on[..., None], blame(rng, on, 0.2, 0.2), -1)
    for r, g, i, k in chains:
        o = np.argsort(-q[r, g, :, i])
        e[r, g, :, i] = -1; e[r, g, o[15], i] = o[0]
        for m in range(k - 1): e[r, g, o[m], i] = o[m + 1]
    return pack(x, n, q, v, e, c, w, t)
def check_inputs(d):
    bad = []
    for k, lo, hi in (("xt", 0, 255), ("nm", 0, W - 1), ("ps", -1, 239), ("dv", 0, D - 1), ("ex", -2, 15), ("dn", 0, W - 1), ("wt", 0, 15), ("th", 0, 4080)):
        v = np.asarray(d[k]).astype(np.float64)
        if not (np.min(v) >= lo and np.max(v) <= hi and np.all(v == np.floor(v))): bad.append("range of " + k)
    if not bad:
        q = d["ps"].astype(np.int64).reshape(N, 8, 16, I); e = d["ex"].astype(np.int64).reshape(N, 8, 16, I, D); s = np.sort(q, axis=2)
        if np.any((s[:, :, 1:] == s[:, :, :-1]) & (s[:, :, 1:] >= 0)): bad.append("equal places in a puzzle of ps")
        if np.any(e == np.arange(16).reshape(1, 1, 16, 1, 1)): bad.append("a variable is its own culprit in ex")
        if np.any((e >= 0) & (np.take_along_axis(q[..., None], np.maximum(e, 0), axis=2) < 0)): bad.append("an unassigned culprit in ex")
    return bad
def reference(xt, nm, ps, dv, ex, dn, wt, th):
    X = xt.astype(np.int32).reshape(N, 8, 16, W); names = nm.astype(np.int64).reshape(N, 8, 16, I); place = ps.astype(np.int64).reshape(N, 8, 16, I)
    value = dv.astype(np.int64).reshape(N, 8, 16, I); expl = ex.astype(np.int64).reshape(N, 8, 16, I, D); dom = dn.astype(np.int64).reshape(N, 8, 16, I, D)
    w = wt.astype(np.int64).reshape(N, 8, 16, 1); thr = th.astype(np.int64).reshape(N, 8, 16, 1)
    pend = np.full((N, 8, I), -1, np.int64); A = [0] * N
    gi = np.arange(8)[:, None]; ii = np.arange(I)[None, :]; rows = np.arange(16)[None, :, None]
    for t in range(T):
        cuts = [0] * N
        for r in range(N):
            s = (r + t) % N
            n, q, v, e, pe, xs = names[r], place[r], value[r], expl[r], pend[r], X[s]
            full = np.all(q >= 0, axis=1); o = np.argmin(q, axis=1)
            p = np.where(pe >= 0, pe, np.where(full, o, np.argmax(q < 0, axis=1)))
            out = full[:, None, :] & (rows == o[:, None, :])
            q[out] = -1; e[out] = -1; e[full[:, None, :, None] & (e == o[:, None, :, None])] = -1
            mine = e[gi, p, ii]
            none = np.all(mine == -2, axis=2); cut = np.all(mine != -1, axis=2) & ~none
            e[(rows == p[:, None, :]) & none[:, None, :]] = -1
            key = np.where(np.any(mine[:, None] == rows[..., None], axis=3), q, -1); j = np.argmax(key, axis=1)
            key = np.where(rows == j[:, None, :], -1, key); j2 = np.where(np.max(key, axis=1) >= 0, np.argmax(key, axis=1), -2)
            g1, i1 = np.nonzero(cut); jj = j[cut]
            e[g1, jj, i1, v[g1, jj, i1]] = j2[cut]
            e[cut[:, None, :, None] & (e == j[:, None, :, None])] = -1
            q[g1, jj, i1] = -1; pe[cut] = jj; p = np.where(cut, j, p); cuts[r] = int(np.count_nonzero(cut))
            free_ = e[gi, p, ii] == -1; has = np.any(free_, axis=2); d = np.argmax(free_, axis=2); c = dom[s][gi, p, ii, d]
            cc = c[:, None, :]; at = ((n * cc >> 5) + n + 37 * cc) & (W - 1)
            xc = np.take_along_axis(xs, cc, 2); y = np.take_along_axis(xs, at.reshape(8, 1, 16 * I), 2).reshape(8, 16, 16, I)
            on = q >= 0
            clash = on & (np.add.reduce(np.abs(y - xc[:, :, None, :]), axis=1) <= thr[s] + 32 * (A[r] & 7)); hit = np.any(clash, axis=1)
            bad = has & hit; g1, i1 = np.nonzero(bad)
            e[g1, p[bad], i1, d[bad]] = np.argmin(np.where(clash, q, 1000), axis=1)[bad]
            ok = has & ~hit; g1, i1 = np.nonzero(ok); pp = p[ok]
            big = np.max(np.where(on[:, None], y, 0), axis=2); h = np.add.reduce(w[s] * big, axis=1) & (B - 1)
            young = np.max(q, axis=1) + 1
            n[g1, pp, i1] = c[ok]; v[g1, pp, i1] = d[ok]; q[g1, pp, i1] = young[ok]; pe[ok] = -1
            xs[g1, :, B * i1 + h[ok]] = ((xc + big) >> 1)[g1, :, i1]
        A = cuts
    shown = np.where(pend[:, :, None, :] == rows[None], -2, place)
    here = [(s - T + 1) % N for s in range(N)]
    return {"yn": names[here].reshape(N, 128, I).astype(np.float32), "yp": shown[here].reshape(N, 128, I).astype(BF), "yd": value[here].reshape(N, 128, I).astype(BF),
            "yg": expl[here].reshape(N, 128, I * D).astype(BF), "yx": X.reshape(N, 128, W).astype(BF)}

@@ -1,0 +1,641 @@
+import math
+import numpy as np
+from concourse.mybir import AluOpType, ActivationFunctionType
+
+ALU = AluOpType
+ACT = ActivationFunctionType
+NV, W, I, H = 6, 4096, 256, 128
+LN2 = math.log(2.0)
+HH = 65536.0
+CK = [HH + 8192.0 * (4 - d) for d in range(4)]
+X0, ZCOL, XW = H, W, H + W + 16 + H
+TINY = -2.0 ** -125
+PATHS = "SSFS"
+XC_ON, PICK_ON, REL_ON, TOP_ON = "S", "S", "S", "SSSS"
+EARLY, RSPLIT = True, 2
+MMAX, GSPLIT, LEAD, TRIES, SEED, WARM = 5000, 2, 8000.0, 2000, 3, 0.003
+TIMES = [(0.5, 1.0, 90.0, 2600.0, 45.0, 70.0, 0.6, 1.56), (0.42, 0.9, 50.0, 2000.0, 15.0, 30.0, 0.5, 1.2), (0.7, 1.15, 150.0, 4000.0, 60.0, 100.0, 1.0, 1.9)]
+WIDE = {"bfloat16": 2, "float16": 2, "uint16": 2, "float32": 4, "int32": 4}
+POOL = {"bfloat16": "pb", "float16": "ph", "uint16": "pu", "float32": "pf", "int32": "pi"}
+
+
+def build(PE_NS, CYC, LAT, RLAT, VFIX, SFIX, TT2, GR):
+    ops, used, slots, hist, tiles, sems = [], {}, {}, {}, [], ["cv", "cs", "ct", "cg", "sent"]
+
+    def view(v, a, b, s=1):
+        return {"buf": v["buf"], "lo": v["lo"] + a * v["st"], "n": (b - a + s - 1) // s, "st": v["st"] * s, "dt": v["dt"], "tile": v["tile"], "key": v["key"]}
+
+    def buf(name, n, dt="bfloat16"):
+        if name not in slots:
+            p = POOL[dt]
+            al = 64 // WIDE[dt]
+            lo = used.get(p, 0)
+            used[p] = lo + (n + al - 1) // al * al
+            slots[name] = {"buf": p, "lo": lo, "n": n, "st": 1, "dt": dt, "tile": None, "key": name}
+        return slots[name]
+
+    def tile(n=512):
+        tiles.append({"acc": [], "bank": None})
+        return {"buf": None, "lo": 0, "n": n, "st": 1, "dt": "float32", "tile": len(tiles) - 1, "key": None}
+
+    def span(v):
+        return v["lo"], v["lo"] + (v["n"] - 1) * v["st"] + 1
+
+    def add(eng, cost, call, rd, wr, lat=LAT, sem=None):
+        me = len(ops)
+        op = {"eng": eng, "cost": cost, "call": call, "deps": set(), "lat": lat, "sem": sem, "alloc": None, "tiles": set()}
+        for v, w in [(x, False) for x in rd] + [(x, True) for x in wr]:
+            if not isinstance(v, dict):
+                continue
+            if v["tile"] is not None:
+                acc = tiles[v["tile"]]["acc"]
+                if not acc:
+                    op["alloc"] = v["tile"]
+                for j, e2, w2 in acc:
+                    if j != me and (w or w2 or e2 != eng) and not eng == e2 == "T":
+                        op["deps"].add(j)
+                    if j != me and eng == e2 == "T":
+                        op["after"] = acc[0][0]
+                acc.append((me, eng, w))
+                op["tiles"].add(v["tile"])
+                continue
+            lo, hi = span(v)
+            lst = hist.setdefault(v["key"], [])
+            for j, l2, h2, w2 in lst:
+                if j != me and l2 < hi and lo < h2 and (w or w2):
+                    op["deps"].add(j)
+            if w and v["st"] == 1:
+                lst[:] = [x for x in lst if not (lo <= x[1] and x[2] <= hi)]
+            lst.append((me, lo, hi, w))
+        ops.append(op)
+        return me
+
+    def narrow(*vs):
+        return all(WIDE[v["dt"]] == 2 and v["tile"] is None for v in vs if isinstance(v, dict))
+
+    def vcost(n, rate):
+        return VFIX + max(64.0, n * rate) * CYC
+
+    def TS(out, a, s1, o1, s2=None, o2=None):
+        add("V", vcost(a["n"], 0.5 if narrow(out, a) else 1.0), ("ts", out, a, s1, s2, o1, o2), [a, s1, s2], [out])
+        return out
+
+    def TT(out, a, b, o):
+        r = (2.0 if a["tile"] is None and b["tile"] is None else 1.0) * (TT2 if narrow(out, a, b) else 1.0)
+        add("V", vcost(a["n"], r), ("tt", out, a, b, o), [a, b], [out])
+        return out
+
+    def CP(out, a):
+        add("V", vcost(a["n"], 1.0), ("cp", out, a), [a], [out])
+        return out
+
+    def SCAN(out, d0, d1, init, o0, o1):
+        add("V", vcost(out["n"], 0.5 if narrow(out, d0, d1) else 1.0), ("scan", out, d0, d1, init, o0, o1), [d0, d1], [out])
+        return out
+
+    def SET(out, c):
+        add("V", vcost(out["n"], 0.5), ("set", out, c), [], [out])
+        return out
+
+    def AC(out, a, f, scale=1.0, bias=0.0, acc=None):
+        add("S", SFIX + max(64.0, a["n"]) * CYC, ("act", out, a, f, scale, bias, acc), [a, scale, bias], [out, acc])
+        return out
+
+    def MM(groups):
+        cost = sum(max(64, r["n"]) * PE_NS + 5.0 for o, ts in groups for l, r in ts)
+        if sum(max(64, r["n"]) for o, ts in groups for l, r in ts) > MMAX and len(groups) > 1:
+            MM(groups[:len(groups) // 2])
+            return MM(groups[len(groups) // 2:])
+        add("T", cost, ("mm", groups), [x for o, ts in groups for t2 in ts for x in t2], [o for o, ts in groups])
+
+    def ACC(early, late, gate=None):
+        for part, first, last in ([(early, True, False), (late, False, True)] if EARLY and gate is not None else [(early + late, True, True)]):
+            cost = sum(max(64, r["n"]) * PE_NS + 5.0 for o, l, r in part)
+            add("T", cost, ("acc", part, first, last), [x for o, l, r in part for x in (l, r)] + [gate], [o for o, l, r in part])
+        return early[0][0]
+
+    def M1(ts, n=H):
+        o = tile(n)
+        MM([(o, ts)])
+        return o
+
+    def GATHER(eng, out, win, off, sub=None):
+        add(eng, 60.0 + out["n"] * GR * CYC, ("gather", eng, out, win, off, sub), [win, off, sub], [out])
+        return out
+
+    def IOTA(out, pat, base, cm):
+        add("G", 130.0 + 2 * out["n"] * CYC, ("iota", out, pat, base, cm), [], [out])
+        return out
+
+    def DMA(kind, v, name, a, b):
+        sem = "d%d" % len(sems)
+        sems.append(sem)
+        lat = 2000.0 + 128 * v["n"] * WIDE[v["dt"]] / 180.0
+        add("D", 60.0, (kind, v, name, a, b, sem), [v] if kind == "store" else [], [v] if kind == "load" else [], lat, sem)
+
+    def SEND(src, dst, hop):
+        sem = "r%d" % len(sems)
+        sems.append(sem)
+        lat = RLAT + 128 * src["n"] * WIDE[src["dt"]] / 70.0
+        j = add("G", 400.0, ("send", src, dst, hop, sem), [src], [], 0.0, "sent")
+        k = add("R", 0.0, ("recv", hop), [], [dst], lat, sem)
+        ops[k]["deps"].add(j)
+
+    X = {"buf": "tab", "lo": 0, "n": XW, "st": 1, "dt": "bfloat16", "tile": None, "key": "tab"}
+    ps_in, dv_in, ex_in = buf("ps_in", I), buf("dv_in", I), buf("ex_in", 4 * I)
+    nm_in, dn_in = buf("nm_in", I, "int32"), buf("dn_in", 4 * I, "int32")
+    wt_in, th_in = buf("wt_in", 1, "int32"), buf("th_in", 1, "int32")
+    for v, name in ((ps_in, "ps"), (ex_in, "ex"), (dn_in, "dn"), (dv_in, "dv"), (nm_in, "nm")):
+        DMA("load", v, name, 0, v["n"])
+    DMA("load", view(X, X0, X0 + W), "xt", 0, W)
+    for v, name in ((wt_in, "wt"), (th_in, "th")):
+        DMA("load", v, name, 0, 1)
+    SET(view(X, X0 + W, X0 + W + 16), 0.0)
+
+    f32 = lambda name, n=1: buf(name, n, "float32")
+    pi_ = IOTA(buf("p_i", 1, "int32"), [[0, 1]], 0, 1)
+    mdiff = IOTA(f32("mdiff", 128), [[1, 128]], 0, -1)
+    mgrp = IOTA(f32("mgrp", 144), [[16, 9], [0, 16]], 0, 0)
+    mvar = IOTA(f32("mvar", 144), [[0, 9], [1, 16]], 0, 0)
+    kc = CP(f32("kc"), TS(buf("k_i", 1, "int32"), pi_, 15, ALU.bitwise_and))
+    gc = CP(f32("gc"), TS(buf("g_i", 1, "int32"), pi_, 112, ALU.bitwise_and))
+    ident = TS(buf("ident", 128), mdiff, 0.0, ALU.is_equal)
+    blk = TS(buf("blk", 128), view(mgrp, 0, 128), gc, ALU.is_equal)
+    ones = SET(buf("ones", 128), 1.0)
+
+    def scaled(base, c, name):
+        if c == 1.0:
+            return base
+        if name not in slots:
+            turn[0] += 1
+            if late[0] and base is ident:
+                add("G", 170.0 + 256 * CYC, ("diag", buf(name, 128), zeros, c), [zeros], [slots[name]])
+            elif turn[0] % 3 == 0:
+                AC(buf(name, 128), base, ACT.Identity, scale=c)
+            else:
+                TS(buf(name, 128), base, c, ALU.mult)
+        return slots[name]
+    turn, late = [0], [False]
+    zeros = SET(buf("zeros", 128), 0.0)
+    sI = lambda c: scaled(ident, float(c), "I%g" % c)
+    sB = lambda c: scaled(blk, float(c), "B%g" % c)
+    col = lambda name, a, b: TS(f32(name), kc, float(a), ALU.mult, float(b), ALU.add)
+    k1, nk1 = col("k1", 1, 1), col("nk1", -1, -1)
+    Bk = scaled(blk, k1, "Bk")
+    Bkh = scaled(blk, col("k1h", 0.5, 0.5), "Bkh")
+    Bk16h = scaled(blk, col("k16", 0.5, -8), "Bk16h")
+    Dk15 = scaled(ident, col("k15", 1, -15), "Dk15")
+    mv = view(mvar, 0, 128)
+    Bp = TT(buf("Bp", 128), TT(buf("c12", 128), TS(buf("c13", 128), mv, 8.0, ALU.mult, 1408.0, ALU.add), blk, ALU.mult), sI(256), ALU.add)
+    IH = TT(buf("IH", 128), ident, sB(0.5), ALU.subtract)
+    Bqh = TT(buf("Bqh", 128), TS(buf("c0", 128), mv, 240.0, ALU.add), sB(0.5), ALU.mult)
+    T2 = TT(buf("T2", 128), TS(buf("c1", 128), mv, 0.0, ALU.is_equal, 8.0, ALU.add), blk, ALU.mult)
+    near = TS(buf("c2", 128), AC(f32("c3", 128), mdiff, ACT.Abs), 1.0, ALU.is_equal)
+    first8 = TS(f32("first8"), kc, 0.0, ALU.is_equal, -8.0, ALU.mult)
+    T1 = TT(buf("T1", 128), TS(buf("c4", 128), TT(buf("c5", 128), near, sI(-2), ALU.add), first8, ALU.add), blk, ALU.mult)
+    Z = TT(buf("Z", 144), TS(buf("c6", 144), mgrp, gc, ALU.is_equal), TS(buf("c7", 144), mvar, 15.0, ALU.is_equal), ALU.mult)
+    Wb = [scaled(blk, TS(f32("wt%d" % h), wt_in, 2.0 * h - 1, ALU.mult), "Wb%d" % h) for h in range(2)]
+    at = TS(buf("c8", 128), mv, kc, ALU.is_equal, 4.0, ALU.mult)
+    Mw = TT(buf("c9", 128), at, TS(buf("c10", 128), mv, k1, ALU.is_equal), ALU.subtract)
+    Mw = AC(f32("Mw", 128), Mw, ACT.Identity, 2.0 ** 19)
+    n15 = TS(f32("n15"), kc, 15.0, ALU.is_lt)
+    fixc = TS(f32("fixc"), n15, 2.0 ** 19, ALU.mult, -32.0, ALU.add)
+    fixh = [TS(f32("fixh%d" % h), n15, 2.0 ** 19, ALU.mult, 61455.0 * (1 - h) - 135.0 * 2 ** 16, ALU.add) for h in range(2)]
+    pw = TS(f32("pw", 8), IOTA(f32("c11", 8), [[16, 8]], 0, 0), kc, ALU.add)
+    c16 = [TS(f32("c160", 8), pw, 16.0, ALU.mult, X0 + 15.0, ALU.add), TS(f32("c161", 8), pw, 16.0, ALU.mult)]
+    spare = [pw, TS(f32("spare", 8), pw, W // 2 + 16.0, ALU.add)]
+    Mneg = SET(buf("Mneg", 512), 0.0)
+    SET(view(Mneg, 0, 512, 16), -1024.0)
+    Mkey = SET(f32("Mkey", 512), 2.0 ** 20)
+    SET(view(Mkey, 0, 512, 4), HH)
+    fused = "F" in PATHS
+    if fused:
+        Mrun = SET(buf("Mrun", 1024), 1.0)
+        SET(view(Mrun, 0, 1024, 16), 0.0)
+        for h in range(2):
+            SET(buf("seed%d" % h, 2048), 0.0)
+    nth = TS(f32("nth"), th_in, -1.0, ALU.mult)
+
+    def top(out, Wt, on):
+        P = M1([(IH, Wt)])
+        if on == "S":
+            return AC(out, P, ACT.Sign, 1.0, TINY)
+        TS(out, P, 0.0, ALU.is_gt, -0.5, ALU.add)
+        return TS(out, out, 2.0, ALU.mult)
+
+    def slot(kind, t, h):
+        sz, sb = buf("%sz%d%d" % (kind, t, h), 4 * H), buf("%sb%d%d" % (kind, t, h), 3 * H)
+        sf, so = buf("%sf%d%d" % (kind, t, h), 3 * H, "float16"), buf("%so%d%d" % (kind, t, h), H + 8, "uint16")
+        return {"sb": sb, "sf": sf, "so": so, "z": sz, "r": view(sb, 0, H), "u": view(sb, H, 2 * H), "D": view(sb, 2 * H, 3 * H), "dn": view(sf, 0, 2 * H),
+                "dv": view(sf, 0, H), "nm": view(sf, H, 2 * H), "mc": view(sf, 2 * H, 3 * H), "off": view(so, 0, H), "offc": view(so, H, H + 8)}
+    pl = lambda v, d: view(v, d * H, (d + 1) * H)
+
+    dn_own, dn_nxt = buf("dn_own", 8 * H, "float16"), buf("dn_nxt", 8 * H, "float16")
+    for h in range(2):
+        TS(view(dn_own, 4 * H * h, 4 * H * (h + 1)), view(dn_in, 4 * H * h, 4 * H * (h + 1)), -2048.0, ALU.add)
+    SEND(dn_own, dn_nxt, -1)
+
+    def logic(t, h, r, z, S, dnc):
+        b = lambda name, n=H, dt="bfloat16": buf("L%s%d%d" % (name, t % 2, h), n, dt)
+        Wo = AC(b("Wo"), r, ACT.Exp, -LN2, 110 * LN2)
+        pf = TT(b("pf"), Wo, M1([(sB(0.5), Wo)]), ALU.is_gt)
+        tt = b("t", 4 * H)
+        if PICK_ON == "V":
+            for d in range(4):
+                TT(pl(tt, d), pl(z, d), pf, ALU.mult)
+        else:
+            PK = tile()
+            MM([(pl(PK, d), [(ident, pl(z, d)), (sI(32), pf)]) for d in range(4)])
+            AC(tt, PK, ACT.Relu, 1.0, -32.0)
+        full = TT(b("full"), pf, TS(b("on"), r, 0.0, ALU.is_ge), ALU.mult)
+        R = b("R", 4 * H)
+        for j in range(RSPLIT):
+            w = 4 * H // RSPLIT
+            AC(view(R, w * j, w * (j + 1)), M1([(blk, view(tt, w * j, w * (j + 1)))], w), ACT.Relu, 1.0, nk1)
+        G = tile(H)
+        ACC([(G, T2, pl(tt, d)) for d in range(4)] + [(G, sB(-64), full)], [(G, T1, pl(R, d)) for d in range(4)], tt)
+        g1 = AC(b("g1"), G, ACT.Relu, -1.0, 33.0)
+        Wm = AC(b("Wm"), M1([(ident, r), (sI(-512), g1)]), ACT.Exp, LN2, -117 * LN2)
+        jf = top(b("jf"), Wm, TOP_ON[0])
+        none = TS(b("none"), M1([(blk, g1), (sI(-64), pf)]), -48.0, ALU.is_equal)
+        dvm = TT(b("dvm"), S["dv"], jf, ALU.mult)
+        tg = b("tg", 4 * H)
+        for d in range(4):
+            TS(pl(tg, d), dvm, 12.0 - d, ALU.is_equal)
+        q = AC(b("q"), M1([(ident, pf), (IH, jf)]), ACT.Identity, 1.0, -7.0)
+        KP = tile()
+        nat = lambda v, d: view(v, d, 4 * H, 4)
+        ACC([(KP, ident, dnc)] + [(nat(KP, d), sI(-65536), pl(z, d)) for d in range(4)],
+            [x for d in range(4) for x in ((nat(KP, d), sI(CK[d]), q), (nat(KP, d), sI(-65536), pl(tg, d)))], g1)
+        key = SCAN(b("key", 4 * H, "float32"), Mkey, KP, HH, ALU.min, ALU.max)
+        m = M1([(ident, nat(dnc, 0)), (sI(CK[0]), full), (sI(CK[0]), none)])
+        TT(m, m, view(key, 3, 4 * H, 4), ALU.max)
+        late[0] = True
+        big = 1.5 * 2.0 ** 36
+        TS(S["D"], m, big, ALU.add, -big, ALU.add)
+        TT(S["mc"], m, S["D"], ALU.subtract)
+        RR = tile(2 * H)
+        MM([(pl(RR, 0), [(sI(119), ones), (sI(-256), full), (Dk15, full), (sI(-136), jf)]),
+            (pl(RR, 1), [(Bp, pf), (Bqh, jf)])])
+        TT(S["r"], pl(RR, 1), TT(b("r1"), pl(RR, 0), r, ALU.min), ALU.max)
+        TS(S["u"], S["r"], -4096.0, ALU.mult, 51.0, ALU.max)
+        CL = tile(2 * H)
+        cP, LP = pl(CL, 0), pl(CL, 1)
+        MM([(cP, [(sI(2080), ones), (blk, S["mc"])]), (LP, [(sI(4096), S["u"]), (sB(101), S["mc"])])])
+        e = TT(b("e", H, "int32"), cP, S["nm"], ALU.mult)
+        TS(e, e, 5, ALU.arith_shift_right, 4095, ALU.bitwise_and)
+        TT(e, LP, e, ALU.add)
+        sc = SCAN(b("sc", H, "float32"), Mw, cP, 0.0, ALU.add, ALU.min)
+        TS(e, e, 0x7F800FFF, ALU.bitwise_and)
+        TS(S["off"], e, float(ZCOL), ALU.min)
+        TS(S["offc"], view(sc, 15, H, 16), fixc, ALU.add)
+        if t > 0:
+            for k in ("so", "sb", "sf"):
+                SEND(S[k], slot("i", t, h)[k], 1)
+        W2 = AC(b("W2"), M1([(ident, r), (sI(-512), g1), (sI(-256), jf)]), ACT.Exp, LN2, -373 * LN2)
+        j2 = top(b("j2"), W2, TOP_ON[1])
+        keep = b("keep", 4 * H)
+        if REL_ON == "V":
+            RP = M1([(sI(68), ones), (Bkh, jf), (Bk, full), (sI(17), none)])
+            for d in range(4):
+                TT(pl(keep, d), RP, pl(z, d), ALU.not_equal)
+        else:
+            rel = AC(b("rel"), M1([(Bkh, jf), (Bk, full), (sI(17), none)]), ACT.Identity, 1.0, 68.0)
+            DF = tile()
+            ACC([(DF, ident, z)], [(pl(DF, d), sI(-1), rel) for d in range(4)])
+            AC(keep, DF, ACT.Abs, 32.0)
+        ZA = tile()
+        ACC([(ZA, ident, z), (ZA, sI(-64), tg)], [(pl(ZA, d), sI(-64), full) for d in range(4)])
+        TT(keep, ZA, keep, ALU.mult if REL_ON == "V" else ALU.min)
+        a2 = AC(b("a2"), M1([(sI(32), full), (sB(8.5), jf), (Bk16h, j2)]), ACT.Identity, 1.0, 36.0)
+        U2 = tile()
+        ACC([(U2, sI(32), tg)], [(pl(U2, d), ident, a2) for d in range(4)])
+        TT(S["z"], U2, keep, ALU.max)
+        if t > 0:
+            SEND(S["z"], slot("i", t, h)["z"], 1)
+        if t < NV - 1:
+            AC(b("junk"), M1([(ones, jf)]), ACT.Identity, 0.5, 64.0, acc=f32("cnt%d%d" % (t, h)))
+            if h == 1:
+                n = TT(buf("cn%d" % t, 1, "int32"), f32("cnt%d0" % t), f32("cnt%d1" % t), ALU.add)
+                TS(n, n, 7, ALU.bitwise_and)
+                SEND(TS(f32("ao%d" % t), n, -32.0, ALU.mult), f32("ai%d" % (t + 1)), 2 if t > 0 else 1)
+
+    def reads(t, h, S, thA):
+        b = lambda name, n=H, dt="bfloat16": buf("G%s%d" % (name, h), n, dt)
+        win = view(X, X0, X0 + W + 16)
+        xc = view(slots["seed%d" % h], 0, 2048, 16) if fused else b("xc")
+        GATHER(XC_ON, xc, win, S["offc"])
+        SP, y, ad, ym = tile(H), b("y", 2048), b("ad", 2048), b("ym", 2048)
+        for c in range(2):
+            path = PATHS[2 * h + c]
+            yc, ac, xcc, off = view(y, 1024 * c, 1024 * (c + 1)), view(ad, 1024 * c, 1024 * (c + 1)), view(xc, 64 * c, 64 * (c + 1)), view(S["off"], 64 * c, 64 * (c + 1))
+            n = 1024 // GSPLIT
+            part = lambda v, j, w: view(v, w * j, w * (j + 1))
+            if path == "F":
+                rep = SCAN(buf("rep%d%d" % (h, c), 1024), Mrun, view(slots["seed%d" % h], 1024 * c, 1024 * (c + 1)), 0.0, ALU.mult, ALU.add)
+                for j in range(GSPLIT):
+                    GATHER("V", part(yc, j, n), win, part(off, j, n // 16), part(rep, j, n))
+                    AC(part(ac, j, n), part(yc, j, n), ACT.Abs)
+                lanes = [view(ac, k, 1024, 16) for k in range(16)]
+            else:
+                for j in range(GSPLIT):
+                    GATHER(path, part(yc, j, n), win, part(off, j, n // 16))
+                for half in range(2):
+                    DP = tile()
+                    MM([(part(DP, j, 64), [(ident, view(yc, 8 * half + j, 1024, 16)), (sI(-1), xcc)]) for j in range(8)])
+                    AC(part(ac, half, 512), DP, ACT.Abs)
+                lanes = [part(ac, k, 64) for k in range(16)]
+            MM([(part(SP, c, 64), [(view(Z, 15 - k, 143 - k), lanes[k]) for k in range(16)])])
+            for j in range(2):
+                SCAN(part(ym, 2 * c + j, 512), Mneg, part(yc, j, 512), -1024.0, ALU.add, ALU.max)
+        nc = AC(b("nc"), SP, ACT.Relu, 1.0, thA)
+        return xc, view(ym, 15, 2048, 16), nc
+
+    def update(t, h, S, got, N_):
+        xc, Y, nc = got
+        b = lambda name, n=H, dt="bfloat16": buf("U%s%d%d" % (name, t % 2, h), n, dt)
+        r = S["r"]
+        Wy = AC(b("Wy"), M1([(ident, r), (sI(-1), S["u"])]), ACT.Exp, LN2, -66 * LN2)
+        npv = AC(b("np"), M1([(ident, r), (sI(256), top(b("ny"), Wy, TOP_ON[2]))]), ACT.Relu, 1.0, -255.0)
+        pen = b("pen", 4 * H)
+        for d in range(4):
+            TS(pl(pen, d), S["D"], CK[d], ALU.not_equal, -2.125, ALU.add)
+        hasn = TS(b("hasn"), S["D"], HH, ALU.is_equal, 8.0, ALU.add)
+        X1 = tile(H)
+        Wc = AC(b("Wc"), ACC([(X1, ident, r), (X1, ident, S["u"])], [(X1, sI(512), nc)], Y), ACT.Exp, -LN2, 174 * LN2)
+        oc = top(b("oc"), Wc, TOP_ON[3])
+        RU = tile(H)
+        r2 = TT(b("r"), ACC([(RU, blk, npv), (RU, sI(-512), hasn)], [(RU, sB(-256), oc)], Wc), r, ALU.max)
+        U5 = tile()
+        ACC([(U5, sI(-32), pen)], [(pl(U5, d), Bkh, oc) for d in range(4)], Wc)
+        z2 = TT(b("z", 4 * H), U5, S["z"], ALU.max)
+        CLP = tile()
+        MM([(pl(CLP, 0), [(sI(1 / 8192), S["D"]), (sI(-16), hasn), (sB(-8), oc)]), (pl(CLP, 1), [(ident, S["mc"]), (sI(-8192), hasn), (sB(-4096), oc)]),
+            (pl(CLP, 2), [(sI(1 / 8192), S["D"]), (sI(16), hasn), (sB(8), oc)]), (pl(CLP, 3), [(ident, S["mc"]), (sI(8192), hasn), (sB(4096), oc)])])
+        TT(N_["dn"], view(CLP, 2 * H, 4 * H), TT(b("n1", 2 * H, "float16"), view(CLP, 0, 2 * H), S["dn"], ALU.max), ALU.min)
+        HV = tile(2 * H)
+        groups = []
+        for c in range(2):
+            s = lambda v: view(v, 64 * c, 64 * (c + 1))
+            f = PATHS[2 * h + c] == "F"
+            groups.append((s(pl(HV, 1)), [(sI(1 if f else 0.5), s(xc)), (sI(0.5), s(Y))]))
+            groups.append((s(pl(HV, 0)), [(sB(2 ** 16), s(hasn)), (Wb[h], s(Y))] + ([(Wb[h], s(xc))] if f else []) + [(sB(2 ** 15), s(oc))]))
+        MM(groups)
+        sh = SCAN(b("sh", H, "float32"), Mw, pl(HV, 0), 140.0 * 2 ** 16, ALU.add, ALU.min)
+        nv = TS(b("nv", H, "int32"), pl(HV, 1), -0.25, ALU.add)
+        hi = TS(b("hi", 8, "int32"), view(sh, 15, H, 16), fixh[h], ALU.add)
+        TS(hi, hi, 0x3000F, ALU.bitwise_and)
+        TT(hi, c16[h], hi, ALU.add if h else ALU.subtract)
+        TT(hi, hi, spare[h], ALU.min if h else ALU.max)
+        return r2, z2, CP(b("so", 8, "uint16"), hi), nv
+
+    def scatter(h, offs, nv):
+        win = view(X, X0 + W // 2, XW) if h else view(X, 0, X0 + W // 2)
+        add("V", 60.0 + H * 3.8 * CYC, ("scatter", win, offs, nv), [offs, nv], [win])
+
+    k16n = col("k16n", -1, 16)
+    for h in range(2):
+        S = slot("i", 0, h)
+        p = view(ps_in, H * h, H * (h + 1))
+        r0 = TT(buf("r0%d" % h, H), TS(buf("r00%d" % h, H), p, k16n, ALU.mult), p, ALU.min)
+        z0, za, zb = buf("z0%d" % h, 4 * H), buf("za%d" % h, 4 * H), buf("zb%d" % h, 4 * H)
+        e = view(ex_in, 4 * H * h, 4 * H * (h + 1))
+        AC(zb, e, ACT.Relu, -18.0, -18.0)
+        ZP = tile()
+        MM([(pl(ZP, d), [(ident, view(e, d, 4 * H, 4)), (ident, view(zb, d, 4 * H, 4))]) for d in range(4)])
+        AC(z0, ZP, ACT.Identity, 1.0, 1.0)
+        TS(S["dv"], view(dv_in, H * h, H * (h + 1)), -1.0, ALU.mult, 12.0, ALU.add)
+        TS(S["nm"], view(nm_in, H * h, H * (h + 1)), -2048.0, ALU.add)
+        logic(0, h, r0, z0, S, view(dn_own, 4 * H * h, 4 * H * (h + 1)))
+
+    yn, yp, yd, yg = f32("yn_s", I), buf("yp_s", I), buf("yd_s", I), buf("yg_s", 4 * I)
+    for t in range(NV):
+        thA = nth if t == 0 else TS(f32("thA%d" % t), f32("ai%d" % t), nth, ALU.add)
+        got = [reads(t, h, slot("i", t, h), thA) for h in range(2)]
+        for h in range(2):
+            N_ = slot("o", t + 1, h)
+            r2, z2, offs, nv = update(t, h, slot("i", t, h), got[h], N_)
+            scatter(h, offs, nv)
+            if t < NV - 1:
+                logic(t + 1, h, r2, z2, N_, view(dn_nxt, 4 * H * h, 4 * H * (h + 1)))
+            else:
+                s = lambda v: view(v, H * h, H * (h + 1))
+                DMA("store", view(X, X0 + W // 2 * h, X0 + W // 2 * (h + 1)), "yx", W // 2 * h, W // 2 * (h + 1))
+                TS(s(yn), N_["nm"], 2048.0, ALU.add)
+                TS(s(yd), N_["dv"], -1.0, ALU.mult, 12.0, ALU.add)
+                TT(s(yp), TS(buf("o1%d" % h, H), r2, -1.0, ALU.max), AC(buf("o2%d" % h, H), r2, ACT.Identity, 1.0, 15.0), ALU.min)
+                zb = AC(slots["zb%d" % h], z2, ACT.Relu, 18.0, -288.0)
+                ZP = tile()
+                MM([(view(ZP, d, 4 * H, 4), [(ident, pl(z2, d)), (sI(-1), pl(zb, d))]) for d in range(4)])
+                og = AC(view(yg, 4 * H * h, 4 * H * (h + 1)), ZP, ACT.Identity, 1.0, -1.0)
+                DMA("store", og, "yg", 4 * H * h, 4 * H * (h + 1))
+                ops[-1]["tail"] = LEAD * (1 - h)
+    for v, name in ((yn, "yn"), (yp, "yp"), (yd, "yd")):
+        DMA("store", v, name, 0, I)
+    return ops, tiles, used, sems
+
+
+def schedule(ops, tiles, costs):
+    n = len(ops)
+    eng, alloc = [o["eng"] for o in ops], [o["alloc"] for o in ops]
+    pred = [sorted(o["deps"] | ({o["after"]} if "after" in o else set())) for o in ops]
+    succ = [[] for _ in ops]
+    for j in range(n):
+        for d in pred[j]:
+            succ[d].append(j)
+    users = [sorted({a[0] for a in t["acc"]}) for t in tiles]
+    cost, lat = costs[0]
+
+    def run(off):
+        prio = [0.0] * n
+        for j in range(n - 1, -1, -1):
+            prio[j] = cost[j] + lat[j] + off.get(kin[j], 0.0) + max([prio[s] for s in succ[j]] + [ops[j].get("tail", 0.0)])
+        left, ready = [len(p) for p in pred], [0.0] * n
+        pool = {e: [j for j in range(n) if not left[j] and eng[j] == e] for e in "VSTGDR"}
+        free = {e: 0.0 for e in pool}
+        todo, end, bank, seq, took = [len(u) for u in users], [0.0] * len(tiles), [None] * 8, [], {}
+        for _ in range(n):
+            room = min([(0.0 if bank[k] is None else end[bank[k]], k) for k in range(8) if bank[k] is None or todo[bank[k]] == 0], default=None)
+            best = None
+            for e, p in pool.items():
+                f = free[e]
+                for j in p:
+                    at = ready[j] if ready[j] > f else f
+                    if alloc[j] is not None:
+                        if room is None:
+                            continue
+                        at = max(at, room[0])
+                    if best is None or (at, -prio[j], j) < best:
+                        best = (at, -prio[j], j)
+            if best is None:
+                return None
+            at, _, j = best
+            e = eng[j]
+            lim, most = at + 0.3 * cost[j], prio[j] + 500.0
+            for i in pool[e]:
+                if ready[i] < lim and prio[i] > most and (alloc[i] is None or (room is not None and room[0] < lim)):
+                    j, most = i, prio[i]
+                    at = max(ready[i], free[e], room[0] if alloc[i] is not None else 0.0)
+            if alloc[j] is not None:
+                took[j] = (room[1], bank[room[1]])
+                bank[room[1]] = alloc[j]
+            pool[e].remove(j)
+            seq.append(j)
+            if e != "R":
+                free[e] = at + cost[j]
+            fin = at + cost[j] + lat[j]
+            for tl in ops[j]["tiles"]:
+                todo[tl] -= 1
+                end[tl] = max(end[tl], fin)
+            for s in succ[j]:
+                ready[s] = max(ready[s], fin)
+                left[s] -= 1
+                if left[s] == 0:
+                    pool[eng[s]].append(s)
+        return seq, took
+
+    def length(seq, took, c, l):
+        fin, free = [0.0] * n, {e: 0.0 for e in "VSTGDR"}
+        for j in seq:
+            at = max([free[eng[j]]] + [fin[d] for d in pred[j]])
+            if j in took and took[j][1] is not None:
+                at = max([at] + [fin[d] for d in users[took[j][1]]])
+            if eng[j] != "R":
+                free[eng[j]] = at + c[j]
+            fin[j] = at + c[j] + l[j]
+        return fin
+
+    sc = [j for j in range(n) if ops[j]["call"][0] == "scatter"]
+    per = sc[4] - sc[2]
+    kin = [j if j < sc[0] or j >= sc[0] + 5 * per else sc[0] + (j - sc[0]) % per for j in range(n)]
+    kinds = sorted(set(kin))
+    rng = np.random.default_rng(SEED)
+    off, plan = {}, run({})
+    base = [max(length(plan[0], plan[1], c, l)) for c, l in costs]
+    best = float(len(costs))
+    now = best
+    for it in range(TRIES):
+        o2 = dict(off)
+        for _ in range(2 ** int(rng.integers(0, 3))):
+            k = kinds[int(rng.integers(0, len(kinds)))]
+            o2[k] = o2.get(k, 0.0) + float(rng.normal()) * (300.0, 1000.0, 3000.0)[int(rng.integers(0, 3))]
+        p2 = run(o2)
+        if p2 is not None:
+            v = sum(max(length(p2[0], p2[1], c, l)) / b for (c, l), b in zip(costs, base))
+            if v <= now + WARM * (1 - it / TRIES) * float(rng.random()):
+                now, off = v, o2
+            if v < best:
+                best, plan = v, p2
+    seq, took = plan
+    for j, (k, old) in took.items():
+        tiles[alloc[j]]["bank"] = k
+        if old is not None:
+            ops[j]["deps"] |= set(users[old])
+    return {e: [j for j in seq if eng[j] == e] for e in "VSTGDR"}, [length(seq, took, c, l) for c, l in costs]
+
+
+OPS, TILES, USED, SEMAPHORES = build(*TIMES[0])
+ORDER, ENDS = schedule(OPS, TILES, [([o["cost"] for o in p], [o["lat"] for o in p]) for p in [build(*t)[0] for t in TIMES]])
+SCRATCH = {"tab": ("sbuf", [128, XW], "bfloat16")}
+SCRATCH.update({p: ("sbuf", [128, USED[p]], d) for d, p in POOL.items()})
+SCRATCH.update({"bank%d" % k: ("psum", [128, 512], "float32") for k in range(8)})
+
+
+def rank_program(g, core, T, topo):
+    rank = T.rank_of(core)
+    if rank is None:
+        return
+    cores = T.cores
+    queue = {"V": g.vector, "S": g.scalar, "T": g.tensor, "G": g, "D": g.sync}
+    counter = {"V": "cv", "S": "cs", "T": "ct", "G": "cg"}
+
+    def ap(v):
+        if not isinstance(v, dict):
+            return v
+        t = T[v["buf"]] if v["tile"] is None else T["bank%d" % TILES[v["tile"]]["bank"]]
+        if v["st"] == 1:
+            return t[:, v["lo"]:v["lo"] + v["n"]]
+        return t[:, v["lo"]:v["lo"] + (v["n"] - 1) * v["st"] + 1:v["st"]]
+
+    mark, sent = {}, 0
+    for e in ORDER:
+        k = 0
+        for j in ORDER[e]:
+            o = OPS[j]
+            if e == "R":
+                mark[j] = (o["sem"], len(topo.engines(cores[(rank - o["call"][1]) % len(cores)], core)))
+            elif e == "D":
+                mark[j] = (o["sem"], 16)
+            elif o["sem"] is None:
+                k += 1
+                mark[j] = (counter[e], k)
+
+    def emit(q, c):
+        kind = c[0]
+        if kind == "ts":
+            if c[6] is None:
+                return q.tensor_scalar(ap(c[1]), ap(c[2]), ap(c[3]), None, c[5])
+            return q.tensor_scalar(ap(c[1]), ap(c[2]), ap(c[3]), ap(c[4]), c[5], c[6])
+        if kind == "tt":
+            return q.tensor_tensor(ap(c[1]), ap(c[2]), ap(c[3]), c[4])
+        if kind == "cp":
+            return q.tensor_copy(ap(c[1]), ap(c[2]))
+        if kind == "scan":
+            return q.tensor_tensor_scan(ap(c[1]), ap(c[2]), ap(c[3]), c[4], c[5], c[6])
+        if kind == "set":
+            return q.memset(ap(c[1]), c[2])
+        if kind == "act":
+            if c[6] is not None:
+                return q.activation(ap(c[1]), ap(c[2]), c[3], bias=c[5], scale=c[4], accum_out=ap(c[6]))
+            return q.activation(ap(c[1]), ap(c[2]), c[3], bias=ap(c[5]), scale=ap(c[4]))
+        if kind == "mm":
+            for out, ts in c[1]:
+                for k, (l, r) in enumerate(ts):
+                    last = q.matmul(ap(out), ap(l), ap(r), k == 0, k == len(ts) - 1)
+            return last
+        if kind == "acc":
+            for k, (out, l, r) in enumerate(c[1]):
+                last = q.matmul(ap(out), ap(l), ap(r), c[2] and k == 0, c[3] and k == len(c[1]) - 1)
+            return last
+        if kind == "gather":
+            src = ap(c[3]).indirect(ap(c[4]))
+            if c[5] is not None:
+                return q.tensor_tensor(ap(c[2]), src, ap(c[5]), ALU.subtract)
+            return q.tensor_copy(ap(c[2]), src) if c[1] == "V" else q.activation(ap(c[2]), src, ACT.Copy)
+        if kind == "scatter":
+            return q.tensor_copy(ap(c[1]).indirect(ap(c[2])), ap(c[3]))
+        if kind == "diag":
+            return q.affine_select(ap(c[1]), ap(c[2]), [[-1, 128]], ALU.not_equal, c[3], 0, 1)
+        if kind == "iota":
+            if c[1]["dt"] == "int32":
+                return q.iota(ap(c[1]), c[2], c[3], c[4])
+            return q.iota(ap(c[1]), c[2], c[3], c[4], allow_small_or_imprecise_dtypes=True)
+        whole = T[c[2]].shape[1] == c[4] - c[3]
+        side = T[c[2]][:] if whole else T[c[2]][:, c[3]:c[4]]
+        return q.dma_start(ap(c[1]), side) if kind == "load" else q.dma_start(side, ap(c[1]))
+
+    for e, q in queue.items():
+        seen = {}
+        for j in ORDER[e]:
+            o = OPS[j]
+            need = {}
+            for d in o["deps"]:
+                s, v = mark[d]
+                need[s] = max(need.get(s, 0), v)
+            for s in sorted(need):
+                if need[s] > seen.get(s, 0):
+                    q.wait_ge(T.sem[s], need[s])
+                    seen[s] = need[s]
+            c = o["call"]
+            if c[0] == "send":
+                dst = cores[(rank + c[3]) % len(cores)]
+                rid, pid, _ = topo.addr(dst)
+                q.remote_dma(ap(c[2]), ap(c[1]), T.sem[c[4]], T.sem["sent"], pid, rid, topo.mask(core, dst))
+                sent += len(topo.engines(core, dst))
+            else:
+                emit(q, c).then_inc(T.sem[mark[j][0]], 16 if e == "D" else 1)
+    last = {"sent": sent}
+    for s, v in mark.values():
+        last[s] = max(last.get(s, 0), v)
+    for s in sorted(last):
+        g.wait_ge(T.sem[s], last[s])

@@ -8,13 +8,17 @@ NV, W, I, H = 6, 4096, 256, 128
 LN2 = math.log(2.0)
 HH = 65536.0
 CK = [HH + 8192.0 * (4 - d) for d in range(4)]
-X0, ZCOL, XW = H, W, H + W + 16 + H
+X0, ZCOL, XW = 0, W, W + 16
 TINY = -2.0 ** -125
 PATHS = "SSFS"
 XC_ON, PICK_ON, REL_ON, TOP_ON = "S", "S", "S", "SSSS"
-EARLY, RSPLIT = True, 2
+EARLY, RSPLIT, PERIOD, REST = True, 2, 22000.0, 12000.0
+NEXTP, DVA, CLV, WMV = 1, 1, 1, 1
 MMAX, GSPLIT, LEAD, TRIES, SEED, WARM = 5000, 2, 8000.0, 2000, 3, 0.003
 TIMES = [(0.5, 1.0, 90.0, 2600.0, 45.0, 70.0, 0.6, 1.56), (0.42, 0.9, 50.0, 2000.0, 15.0, 30.0, 0.5, 1.2), (0.7, 1.15, 150.0, 4000.0, 60.0, 100.0, 1.0, 1.9)]
+TIMES = [(0.54, 1.08, 200.0, 3500.0, 65.0, 85.0, 0.6, 1.9), (0.42, 0.83, 170.0, 3000.0, 50.0, 65.0, 0.5, 1.56), (0.8, 1.15, 200.0, 4000.0, 75.0, 100.0, 0.6, 1.8)]
+PATHS, REL_ON, PICK_ON, PERIOD, TRIES, NV_ON, SEED, WARM = "SSFS", "V", "V", 0, 1800, "S", 1, 0.006
+NEXTP, DVA, CLV, WMV = 0, 0, 1, 0
 WIDE = {"bfloat16": 2, "float16": 2, "uint16": 2, "float32": 4, "int32": 4}
 POOL = {"bfloat16": "pb", "float16": "ph", "uint16": "pu", "float32": "pf", "int32": "pi"}
 
@@ -145,7 +149,10 @@ def build(PE_NS, CYC, LAT, RLAT, VFIX, SFIX, TT2, GR):
     ps_in, dv_in, ex_in = buf("ps_in", I), buf("dv_in", I), buf("ex_in", 4 * I)
     nm_in, dn_in = buf("nm_in", I, "int32"), buf("dn_in", 4 * I, "int32")
     wt_in, th_in = buf("wt_in", 1, "int32"), buf("th_in", 1, "int32")
-    for v, name in ((ps_in, "ps"), (ex_in, "ex"), (dn_in, "dn"), (dv_in, "dv"), (nm_in, "nm")):
+    DMA("load", view(ex_in, 0, 2 * I), "ex", 0, 2 * I)
+    DMA("load", ps_in, "ps", 0, I)
+    DMA("load", view(ex_in, 2 * I, 4 * I), "ex", 2 * I, 4 * I)
+    for v, name in ((dv_in, "dv"), (dn_in, "dn"), (nm_in, "nm")):
         DMA("load", v, name, 0, v["n"])
     DMA("load", view(X, X0, X0 + W), "xt", 0, W)
     for v, name in ((wt_in, "wt"), (th_in, "th")):
@@ -188,24 +195,23 @@ def build(PE_NS, CYC, LAT, RLAT, VFIX, SFIX, TT2, GR):
     mv = view(mvar, 0, 128)
     Bp = TT(buf("Bp", 128), TT(buf("c12", 128), TS(buf("c13", 128), mv, 8.0, ALU.mult, 1408.0, ALU.add), blk, ALU.mult), sI(256), ALU.add)
     IH = TT(buf("IH", 128), ident, sB(0.5), ALU.subtract)
+    I7 = TT(buf("I7", 128), ident, sB(7), ALU.subtract) if DVA else None
+    IB = TT(buf("IB", 128), sI(512), sB(512), ALU.subtract) if NEXTP else None
     Bqh = TT(buf("Bqh", 128), TS(buf("c0", 128), mv, 240.0, ALU.add), sB(0.5), ALU.mult)
     T2 = TT(buf("T2", 128), TS(buf("c1", 128), mv, 0.0, ALU.is_equal, 8.0, ALU.add), blk, ALU.mult)
     near = TS(buf("c2", 128), AC(f32("c3", 128), mdiff, ACT.Abs), 1.0, ALU.is_equal)
     first8 = TS(f32("first8"), kc, 0.0, ALU.is_equal, -8.0, ALU.mult)
     T1 = TT(buf("T1", 128), TS(buf("c4", 128), TT(buf("c5", 128), near, sI(-2), ALU.add), first8, ALU.add), blk, ALU.mult)
     Z = TT(buf("Z", 144), TS(buf("c6", 144), mgrp, gc, ALU.is_equal), TS(buf("c7", 144), mvar, 15.0, ALU.is_equal), ALU.mult)
-    Wb = [scaled(blk, TS(f32("wt%d" % h), wt_in, 2.0 * h - 1, ALU.mult), "Wb%d" % h) for h in range(2)]
+    Wb = scaled(blk, CP(f32("wt"), wt_in), "Wb")
     at = TS(buf("c8", 128), mv, kc, ALU.is_equal, 4.0, ALU.mult)
     Mw = TT(buf("c9", 128), at, TS(buf("c10", 128), mv, k1, ALU.is_equal), ALU.subtract)
     Mw = AC(f32("Mw", 128), Mw, ACT.Identity, 2.0 ** 19)
     n15 = TS(f32("n15"), kc, 15.0, ALU.is_lt)
     fixc = TS(f32("fixc"), n15, 2.0 ** 19, ALU.mult, -32.0, ALU.add)
-    fixh = [TS(f32("fixh%d" % h), n15, 2.0 ** 19, ALU.mult, 61455.0 * (1 - h) - 135.0 * 2 ** 16, ALU.add) for h in range(2)]
-    pw = TS(f32("pw", 8), IOTA(f32("c11", 8), [[16, 8]], 0, 0), kc, ALU.add)
-    c16 = [TS(f32("c160", 8), pw, 16.0, ALU.mult, X0 + 15.0, ALU.add), TS(f32("c161", 8), pw, 16.0, ALU.mult)]
-    spare = [pw, TS(f32("spare", 8), pw, W // 2 + 16.0, ALU.add)]
-    Mneg = SET(buf("Mneg", 512), 0.0)
-    SET(view(Mneg, 0, 512, 16), -1024.0)
+    c16 = TS(f32("c16", 8), IOTA(f32("c11", 8), [[16, 8]], 0, 0), kc, ALU.add, 16.0, ALU.mult)
+    Mneg = SET(buf("Mneg", 1024), 0.0)
+    SET(view(Mneg, 0, 1024, 16), -1024.0)
     Mkey = SET(f32("Mkey", 512), 2.0 ** 20)
     SET(view(Mkey, 0, 512, 4), HH)
     fused = "F" in PATHS
@@ -214,7 +220,7 @@ def build(PE_NS, CYC, LAT, RLAT, VFIX, SFIX, TT2, GR):
         SET(view(Mrun, 0, 1024, 16), 0.0)
         for h in range(2):
             SET(buf("seed%d" % h, 2048), 0.0)
-    nth = TS(f32("nth"), th_in, -1.0, ALU.mult)
+    nth = TS(f32("nth"), th_in, -1.0, ALU.mult, -102.0, ALU.add)
 
     def top(out, Wt, on):
         P = M1([(IH, Wt)])
@@ -224,9 +230,9 @@ def build(PE_NS, CYC, LAT, RLAT, VFIX, SFIX, TT2, GR):
         return TS(out, out, 2.0, ALU.mult)
 
     def slot(kind, t, h):
-        sz, sb = buf("%sz%d%d" % (kind, t, h), 4 * H), buf("%sb%d%d" % (kind, t, h), 3 * H)
+        sz, sb = buf("%sz%d%d" % (kind, t, h), 4 * H), buf("%sb%d%d" % (kind, t, h), (3 + NEXTP) * H)
         sf, so = buf("%sf%d%d" % (kind, t, h), 3 * H, "float16"), buf("%so%d%d" % (kind, t, h), H + 8, "uint16")
-        return {"sb": sb, "sf": sf, "so": so, "z": sz, "r": view(sb, 0, H), "u": view(sb, H, 2 * H), "D": view(sb, 2 * H, 3 * H), "dn": view(sf, 0, 2 * H),
+        return {"sb": sb, "sf": sf, "so": so, "z": sz, "r": view(sb, 0, H), "u": view(sb, H, 2 * H), "D": view(sb, 2 * H, 3 * H), "q": view(sb, 3 * H, 4 * H), "dn": view(sf, 0, 2 * H),
                 "dv": view(sf, 0, H), "nm": view(sf, H, 2 * H), "mc": view(sf, 2 * H, 3 * H), "off": view(so, 0, H), "offc": view(so, H, H + 8)}
     pl = lambda v, d: view(v, d * H, (d + 1) * H)
 
@@ -235,10 +241,19 @@ def build(PE_NS, CYC, LAT, RLAT, VFIX, SFIX, TT2, GR):
         TS(view(dn_own, 4 * H * h, 4 * H * (h + 1)), view(dn_in, 4 * H * h, 4 * H * (h + 1)), -2048.0, ALU.add)
     SEND(dn_own, dn_nxt, -1)
 
-    def logic(t, h, r, z, S, dnc):
+    def held(name, dv, u):
+        x, out = TT(buf(name + "x", H), dv, u, ALU.subtract), buf(name, 4 * H)
+        for d in range(4):
+            TS(pl(out, d), x, 12.0 - d - 51.0, ALU.is_equal)
+        return out
+
+    def logic(t, h, r, z, S, dnc, pf, dA):
         b = lambda name, n=H, dt="bfloat16": buf("L%s%d%d" % (name, t % 2, h), n, dt)
-        Wo = AC(b("Wo"), r, ACT.Exp, -LN2, 110 * LN2)
-        pf = TT(b("pf"), Wo, M1([(sB(0.5), Wo)]), ALU.is_gt)
+        if pf is None:
+            Wo = AC(b("Wo"), r, ACT.Exp, -LN2, 110 * LN2)
+            pf = TT(b("pf"), Wo, M1([(sB(0.5), Wo)]), ALU.is_gt)
+        if WMV:
+            Wy = AC(b("Wy"), r, ACT.Exp, LN2, -117 * LN2)
         tt = b("t", 4 * H)
         if PICK_ON == "V":
             for d in range(4):
@@ -247,26 +262,36 @@ def build(PE_NS, CYC, LAT, RLAT, VFIX, SFIX, TT2, GR):
             PK = tile()
             MM([(pl(PK, d), [(ident, pl(z, d)), (sI(32), pf)]) for d in range(4)])
             AC(tt, PK, ACT.Relu, 1.0, -32.0)
-        full = TT(b("full"), pf, TS(b("on"), r, 0.0, ALU.is_ge), ALU.mult)
+        full = TT(b("full"), pf, AC(b("on"), r, ACT.Relu, 1.0, 1.0), ALU.min)
         R = b("R", 4 * H)
         for j in range(RSPLIT):
             w = 4 * H // RSPLIT
             AC(view(R, w * j, w * (j + 1)), M1([(blk, view(tt, w * j, w * (j + 1)))], w), ACT.Relu, 1.0, nk1)
         G = tile(H)
         ACC([(G, T2, pl(tt, d)) for d in range(4)] + [(G, sB(-64), full)], [(G, T1, pl(R, d)) for d in range(4)], tt)
+        if WMV:
+            Wm = TT(b("Wm"), TS(b("fl"), G, 33.0, ALU.is_ge), Wy, ALU.mult)
         g1 = AC(b("g1"), G, ACT.Relu, -1.0, 33.0)
-        Wm = AC(b("Wm"), M1([(ident, r), (sI(-512), g1)]), ACT.Exp, LN2, -117 * LN2)
+        if not WMV:
+            Wm = AC(b("Wm"), M1([(ident, r), (sI(-512), g1)]), ACT.Exp, LN2, -117 * LN2)
         jf = top(b("jf"), Wm, TOP_ON[0])
         none = TS(b("none"), M1([(blk, g1), (sI(-64), pf)]), -48.0, ALU.is_equal)
         dvm = TT(b("dvm"), S["dv"], jf, ALU.mult)
         tg = b("tg", 4 * H)
         for d in range(4):
             TS(pl(tg, d), dvm, 12.0 - d, ALU.is_equal)
-        q = AC(b("q"), M1([(ident, pf), (IH, jf)]), ACT.Identity, 1.0, -7.0)
+        if dA is None or (NEXTP and t < NV - 1):
+            q = AC(S["q"] if NEXTP else b("q"), M1([(ident, pf), (IH, jf)]), ACT.Relu, 1.0, -7.0)
+        elif NEXTP:
+            AC(S["q"], pf, ACT.Identity)
         KP = tile()
         nat = lambda v, d: view(v, d, 4 * H, 4)
-        ACC([(KP, ident, dnc)] + [(nat(KP, d), sI(-65536), pl(z, d)) for d in range(4)],
-            [x for d in range(4) for x in ((nat(KP, d), sI(CK[d]), q), (nat(KP, d), sI(-65536), pl(tg, d)))], g1)
+        early = [(KP, ident, dnc)] + [(nat(KP, d), sI(-65536), pl(z, d)) for d in range(4)]
+        if dA is None:
+            ACC(early, [x for d in range(4) for x in ((nat(KP, d), sI(CK[d]), q), (nat(KP, d), sI(-65536), pl(tg, d)))], g1)
+        else:
+            ACC(early + [x for d in range(4) for x in ((nat(KP, d), sI(-65536), pl(dA, d)), (nat(KP, d), scaled(I7, CK[d], "I7%d" % d), pf))],
+                [(nat(KP, d), scaled(IH, CK[d], "IH%d" % d), jf) for d in range(4)], R)
         key = SCAN(b("key", 4 * H, "float32"), Mkey, KP, HH, ALU.min, ALU.max)
         m = M1([(ident, nat(dnc, 0)), (sI(CK[0]), full), (sI(CK[0]), none)])
         TT(m, m, view(key, 3, 4 * H, 4), ALU.max)
@@ -345,10 +370,9 @@ def build(PE_NS, CYC, LAT, RLAT, VFIX, SFIX, TT2, GR):
                     MM([(part(DP, j, 64), [(ident, view(yc, 8 * half + j, 1024, 16)), (sI(-1), xcc)]) for j in range(8)])
                     AC(part(ac, half, 512), DP, ACT.Abs)
                 lanes = [part(ac, k, 64) for k in range(16)]
-            MM([(part(SP, c, 64), [(view(Z, 15 - k, 143 - k), lanes[k]) for k in range(16)])])
-            for j in range(2):
-                SCAN(part(ym, 2 * c + j, 512), Mneg, part(yc, j, 512), -1024.0, ALU.add, ALU.max)
-        nc = AC(b("nc"), SP, ACT.Relu, 1.0, thA)
+            MM([(part(SP, c, 64), [(sI(2), part(S["u"], c, 64))] + [(view(Z, 15 - k, 143 - k), lanes[k]) for k in range(16)])])
+            SCAN(part(ym, c, 1024), Mneg, yc, -1024.0, ALU.add, ALU.max)
+        nc = TS(b("nc"), SP, thA, ALU.add, 0.0, ALU.is_le) if CLV else AC(b("nc"), SP, ACT.Relu, 1.0, thA)
         return xc, view(ym, 15, 2048, 16), nc
 
     def update(t, h, S, got, N_):
@@ -361,36 +385,59 @@ def build(PE_NS, CYC, LAT, RLAT, VFIX, SFIX, TT2, GR):
         for d in range(4):
             TS(pl(pen, d), S["D"], CK[d], ALU.not_equal, -2.125, ALU.add)
         hasn = TS(b("hasn"), S["D"], HH, ALU.is_equal, 8.0, ALU.add)
+        has0 = AC(b("has0"), hasn, ACT.Identity, 1.0, -8.9375)
         X1 = tile(H)
-        Wc = AC(b("Wc"), ACC([(X1, ident, r), (X1, ident, S["u"])], [(X1, sI(512), nc)], Y), ACT.Exp, -LN2, 174 * LN2)
+        ahead = NEXTP and t < NV - 1
+        early = [(X1, ident, r), (X1, ident, S["u"])] + ([(X1, sB(512), has0)] if ahead else [])
+        if CLV:
+            Wc = TT(b("Wc"), AC(b("Wo"), ACC(early, []), ACT.Exp, -LN2, 174 * LN2), nc, ALU.mult)
+        else:
+            Wc = AC(b("Wc"), ACC(early, [(X1, sI(512), nc)], Y), ACT.Exp, -LN2, 174 * LN2)
         oc = top(b("oc"), Wc, TOP_ON[3])
+        dA = held("UdA%d%d" % (t % 2, h), S["dv"], S["u"]) if DVA and t < NV - 1 else None
+        pf = None
+        if ahead:
+            rA = TT(b("rA"), M1([(blk, npv), (IB, S["q"])]), r, ALU.max)
+            WA = AC(b("WA"), rA, ACT.Exp, -LN2, 110 * LN2)
+            pA = TT(b("pA"), WA, M1([(sB(0.5), WA)]), ALU.is_gt)
+            PF = tile(H)
+            pf = TS(b("pf"), ACC([(PF, ident, S["q"]), (PF, sI(-1), pA), (PF, sB(-2), hasn)], [(PF, sB(-1), oc)], Wc), -271.0, ALU.is_equal)
         RU = tile(H)
         r2 = TT(b("r"), ACC([(RU, blk, npv), (RU, sI(-512), hasn)], [(RU, sB(-256), oc)], Wc), r, ALU.max)
         U5 = tile()
         ACC([(U5, sI(-32), pen)], [(pl(U5, d), Bkh, oc) for d in range(4)], Wc)
         z2 = TT(b("z", 4 * H), U5, S["z"], ALU.max)
         CLP = tile()
-        MM([(pl(CLP, 0), [(sI(1 / 8192), S["D"]), (sI(-16), hasn), (sB(-8), oc)]), (pl(CLP, 1), [(ident, S["mc"]), (sI(-8192), hasn), (sB(-4096), oc)]),
-            (pl(CLP, 2), [(sI(1 / 8192), S["D"]), (sI(16), hasn), (sB(8), oc)]), (pl(CLP, 3), [(ident, S["mc"]), (sI(8192), hasn), (sB(4096), oc)])])
+        nok = AC(b("nok"), M1([(ident, hasn), (sB(0.5), oc)]), ACT.Identity)
+        MM([(pl(CLP, 0), [(sI(1 / 8192), S["D"]), (sI(-16), nok)]), (pl(CLP, 1), [(ident, S["mc"]), (sI(-8192), nok)]),
+            (pl(CLP, 2), [(sI(1 / 8192), S["D"]), (sI(16), nok)]), (pl(CLP, 3), [(ident, S["mc"]), (sI(8192), nok)])])
         TT(N_["dn"], view(CLP, 2 * H, 4 * H), TT(b("n1", 2 * H, "float16"), view(CLP, 0, 2 * H), S["dn"], ALU.max), ALU.min)
         HV = tile(2 * H)
         groups = []
         for c in range(2):
             s = lambda v: view(v, 64 * c, 64 * (c + 1))
             f = PATHS[2 * h + c] == "F"
-            groups.append((s(pl(HV, 1)), [(sI(1 if f else 0.5), s(xc)), (sI(0.5), s(Y))]))
-            groups.append((s(pl(HV, 0)), [(sB(2 ** 16), s(hasn)), (Wb[h], s(Y))] + ([(Wb[h], s(xc))] if f else []) + [(sB(2 ** 15), s(oc))]))
+            groups.append((s(pl(HV, 1)), [(sI(-0.25), s(ones)), (sI(1 if f else 0.5), s(xc)), (sI(0.5), s(Y))]))
+            groups.append((s(pl(HV, 0)), ([(Wb, s(xc))] if f else []) + [(Wb, s(Y))]))
         MM(groups)
-        sh = SCAN(b("sh", H, "float32"), Mw, pl(HV, 0), 140.0 * 2 ** 16, ALU.add, ALU.min)
-        nv = TS(b("nv", H, "int32"), pl(HV, 1), -0.25, ALU.add)
-        hi = TS(b("hi", 8, "int32"), view(sh, 15, H, 16), fixh[h], ALU.add)
-        TS(hi, hi, 0x3000F, ALU.bitwise_and)
-        TT(hi, c16[h], hi, ALU.add if h else ALU.subtract)
-        TT(hi, hi, spare[h], ALU.min if h else ALU.max)
-        return r2, z2, CP(b("so", 8, "uint16"), hi), nv
+        sh = SCAN(b("sh", H, "float32"), Mw, pl(HV, 0), 0.0, ALU.add, ALU.min)
+        big = 1.5 * 2.0 ** 23
+        if NV_ON == "V":
+            nv = TS(b("nv"), pl(HV, 1), big, ALU.add, -big, ALU.add)
+        else:
+            nv = AC(b("nv"), AC(b("nw", H, "float32"), pl(HV, 1), ACT.Identity, 1.0, big), ACT.Identity, 1.0, -big)
+        hi = CP(b("hi", 8, "int32"), view(sh, 15, H, 16))
+        TS(hi, hi, 15, ALU.bitwise_and)
+        offs = CP(b("so", 8, "uint16"), TT(hi, c16, hi, ALU.add))
+        val = GATHER(XC_ON, b("old"), view(X, W // 2 * h, W // 2 * (h + 1)), offs)
+        for sign, o in ((-1, ALU.max), (1, ALU.min)):
+            P = tile(H)
+            ACC([(P, ident, nv), (P, sB(256 * sign), has0)], [(P, sB(256 * sign), nc)], nv)
+            val = TT(b("val%d" % sign), P, val, o)
+        return r2, z2, pf, dA, offs, val
 
     def scatter(h, offs, nv):
-        win = view(X, X0 + W // 2, XW) if h else view(X, 0, X0 + W // 2)
+        win = view(X, W // 2 * h, W // 2 * (h + 1))
         add("V", 60.0 + H * 3.8 * CYC, ("scatter", win, offs, nv), [offs, nv], [win])
 
     k16n = col("k16n", -1, 16)
@@ -406,18 +453,23 @@ def build(PE_NS, CYC, LAT, RLAT, VFIX, SFIX, TT2, GR):
         AC(z0, ZP, ACT.Identity, 1.0, 1.0)
         TS(S["dv"], view(dv_in, H * h, H * (h + 1)), -1.0, ALU.mult, 12.0, ALU.add)
         TS(S["nm"], view(nm_in, H * h, H * (h + 1)), -2048.0, ALU.add)
-        logic(0, h, r0, z0, S, view(dn_own, 4 * H * h, 4 * H * (h + 1)))
+        logic(0, h, r0, z0, S, view(dn_own, 4 * H * h, 4 * H * (h + 1)), None, None)
 
     yn, yp, yd, yg = f32("yn_s", I), buf("yp_s", I), buf("yd_s", I), buf("yg_s", 4 * I)
     for t in range(NV):
         thA = nth if t == 0 else TS(f32("thA%d" % t), f32("ai%d" % t), nth, ALU.add)
-        got = [reads(t, h, slot("i", t, h), thA) for h in range(2)]
+        got = []
+        for h in range(2):
+            first = len(ops)
+            got.append(reads(t, h, slot("i", t, h), thA))
+            for j, o in enumerate(x for x in ops[first:] if x["call"][0] == "gather" and PERIOD):
+                o["due"] = (NV - 1 - t) * PERIOD + (1 - h) * LEAD + REST - 500.0 * j
         for h in range(2):
             N_ = slot("o", t + 1, h)
-            r2, z2, offs, nv = update(t, h, slot("i", t, h), got[h], N_)
+            r2, z2, pf, dA, offs, nv = update(t, h, slot("i", t, h), got[h], N_)
             scatter(h, offs, nv)
             if t < NV - 1:
-                logic(t + 1, h, r2, z2, N_, view(dn_nxt, 4 * H * h, 4 * H * (h + 1)))
+                logic(t + 1, h, r2, z2, N_, view(dn_nxt, 4 * H * h, 4 * H * (h + 1)), pf, dA)
             else:
                 s = lambda v: view(v, H * h, H * (h + 1))
                 DMA("store", view(X, X0 + W // 2 * h, X0 + W // 2 * (h + 1)), "yx", W // 2 * h, W // 2 * (h + 1))
@@ -449,7 +501,10 @@ def schedule(ops, tiles, costs):
     def run(off):
         prio = [0.0] * n
         for j in range(n - 1, -1, -1):
-            prio[j] = cost[j] + lat[j] + off.get(kin[j], 0.0) + max([prio[s] for s in succ[j]] + [ops[j].get("tail", 0.0)])
+            if "due" in ops[j]:
+                prio[j] = ops[j]["due"] + off.get(kin[j], 0.0)
+            else:
+                prio[j] = cost[j] + lat[j] + off.get(kin[j], 0.0) + max([prio[s] for s in succ[j]] + [ops[j].get("tail", 0.0)])
         left, ready = [len(p) for p in pred], [0.0] * n
         pool = {e: [j for j in range(n) if not left[j] and eng[j] == e] for e in "VSTGDR"}
         free = {e: 0.0 for e in pool}

@@ -1,30 +1,28 @@
 import math
 import numpy as np
+from concourse.bass import DstId, RemoteDMATransfer
 from concourse.mybir import AluOpType, ActivationFunctionType
 
 ALU = AluOpType
 ACT = ActivationFunctionType
 NV, W, I, H = 6, 4096, 256, 128
 LN2 = math.log(2.0)
-HH = 65536.0
-CK = [HH + 8192.0 * (4 - d) for d in range(4)]
-X0, ZCOL, XW = 0, W, W + 16
-TINY = -2.0 ** -125
-PATHS = "SSFS"
-XC_ON, PICK_ON, REL_ON, TOP_ON = "S", "S", "S", "SSSS"
-EARLY, RSPLIT, PERIOD, REST = True, 2, 22000.0, 12000.0
-NEXTP, DVA, CLV, WMV = 1, 1, 1, 1
-MMAX, GSPLIT, LEAD, TRIES, SEED, WARM = 5000, 2, 8000.0, 2000, 3, 0.003
-TIMES = [(0.5, 1.0, 90.0, 2600.0, 45.0, 70.0, 0.6, 1.56), (0.42, 0.9, 50.0, 2000.0, 15.0, 30.0, 0.5, 1.2), (0.7, 1.15, 150.0, 4000.0, 60.0, 100.0, 1.0, 1.9)]
-TIMES = [(0.54, 1.08, 200.0, 3500.0, 65.0, 85.0, 0.6, 1.9), (0.42, 0.83, 170.0, 3000.0, 50.0, 65.0, 0.5, 1.56), (0.8, 1.15, 200.0, 4000.0, 75.0, 100.0, 0.6, 1.8)]
-PATHS, REL_ON, PICK_ON, PERIOD, TRIES, NV_ON, SEED, WARM = "SSFS", "V", "V", 0, 1800, "S", 1, 0.006
-NEXTP, DVA, CLV, WMV = 0, 0, 1, 0
+CK = [8192.0 * (4 - d) for d in range(4)]
+SPARE = 4160
+ZCOL, XW = W, W + SPARE
+TINY = -2.0 ** -126
+HELD = 64.0
+OPT = {"paths": "SSFS", "xc": "S", "pick": "V", "pfs": 1, "turn": 8, "wraph": "V", "wrapc": "V", "nv": "V", "full": "V", "nok": "V", "nokb": "S", "pen": "V",
+       "nm": "V", "rsplit": 2, "gsplit": 2, "spare": 2, "b": "V", "wc": "V"}
+LEAD, TRIES, SEED, WARM = 8000.0, 3000, 1, 0.006
+TIMES = [(0.45, 0.85, 130.0, 2600.0, 50.0, 65.0, 0.5, 1.56), (0.55, 1.05, 180.0, 3300.0, 60.0, 80.0, 0.5, 1.7), (0.65, 1.25, 200.0, 4000.0, 75.0, 100.0, 0.5, 1.9)]
 WIDE = {"bfloat16": 2, "float16": 2, "uint16": 2, "float32": 4, "int32": 4}
 POOL = {"bfloat16": "pb", "float16": "ph", "uint16": "pu", "float32": "pf", "int32": "pi"}
 
 
 def build(PE_NS, CYC, LAT, RLAT, VFIX, SFIX, TT2, GR):
-    ops, used, slots, hist, tiles, sems = [], {}, {}, {}, [], ["cv", "cs", "ct", "cg", "sent"]
+    ops, used, slots, hist, tiles, sems = [], {}, {}, {}, [], ["cv", "cs", "ct", "cg"]
+    phase, paths = [None, 0], OPT["paths"]
 
     def view(v, a, b, s=1):
         return {"buf": v["buf"], "lo": v["lo"] + a * v["st"], "n": (b - a + s - 1) // s, "st": v["st"] * s, "dt": v["dt"], "tile": v["tile"], "key": v["key"]}
@@ -45,9 +43,12 @@ def build(PE_NS, CYC, LAT, RLAT, VFIX, SFIX, TT2, GR):
     def span(v):
         return v["lo"], v["lo"] + (v["n"] - 1) * v["st"] + 1
 
-    def add(eng, cost, call, rd, wr, lat=LAT, sem=None):
+    def add(eng, cost, call, rd, wr, lat=LAT, sem=None, alone=False):
         me = len(ops)
-        op = {"eng": eng, "cost": cost, "call": call, "deps": set(), "lat": lat, "sem": sem, "alloc": None, "tiles": set()}
+        op = {"eng": eng, "cost": cost, "call": call, "deps": set(), "lat": lat, "sem": sem, "alloc": None, "tiles": set(), "kin": ("", me)}
+        if phase[0] is not None and not alone:
+            phase[1] += 1
+            op["kin"] = tuple(phase)
         for v, w in [(x, False) for x in rd] + [(x, True) for x in wr]:
             if not isinstance(v, dict):
                 continue
@@ -59,7 +60,7 @@ def build(PE_NS, CYC, LAT, RLAT, VFIX, SFIX, TT2, GR):
                     if j != me and (w or w2 or e2 != eng) and not eng == e2 == "T":
                         op["deps"].add(j)
                     if j != me and eng == e2 == "T":
-                        op["after"] = acc[0][0]
+                        op["after"] = j
                 acc.append((me, eng, w))
                 op["tiles"].add(v["tile"])
                 continue
@@ -80,8 +81,8 @@ def build(PE_NS, CYC, LAT, RLAT, VFIX, SFIX, TT2, GR):
     def vcost(n, rate):
         return VFIX + max(64.0, n * rate) * CYC
 
-    def TS(out, a, s1, o1, s2=None, o2=None):
-        add("V", vcost(a["n"], 0.5 if narrow(out, a) else 1.0), ("ts", out, a, s1, s2, o1, o2), [a, s1, s2], [out])
+    def TS(out, a, s1, o1, s2=None, o2=None, alone=False):
+        add("V", vcost(a["n"], 0.5 if narrow(out, a) else 1.0), ("ts", out, a, s1, s2, o1, o2), [a, s1, s2], [out], alone=alone)
         return out
 
     def TT(out, a, b, o):
@@ -101,27 +102,30 @@ def build(PE_NS, CYC, LAT, RLAT, VFIX, SFIX, TT2, GR):
         add("V", vcost(out["n"], 0.5), ("set", out, c), [], [out])
         return out
 
-    def AC(out, a, f, scale=1.0, bias=0.0, acc=None):
-        add("S", SFIX + max(64.0, a["n"]) * CYC, ("act", out, a, f, scale, bias, acc), [a, scale, bias], [out, acc])
+    def AC(out, a, f, scale=1.0, bias=0.0, acc=None, alone=False):
+        add("S", SFIX + max(64.0, a["n"]) * CYC, ("act", out, a, f, scale, bias, acc), [a, scale, bias], [out, acc], alone=alone)
         return out
 
-    def MM(groups):
-        cost = sum(max(64, r["n"]) * PE_NS + 5.0 for o, ts in groups for l, r in ts)
-        if sum(max(64, r["n"]) for o, ts in groups for l, r in ts) > MMAX and len(groups) > 1:
-            MM(groups[:len(groups) // 2])
-            return MM(groups[len(groups) // 2:])
-        add("T", cost, ("mm", groups), [x for o, ts in groups for t2 in ts for x in t2], [o for o, ts in groups])
+    def mcost(r):
+        return max(64, r["n"]) * PE_NS * (4 if r["dt"] == "float32" else 1) + 5.0
 
-    def ACC(early, late, gate=None):
-        for part, first, last in ([(early, True, False), (late, False, True)] if EARLY and gate is not None else [(early + late, True, True)]):
-            cost = sum(max(64, r["n"]) * PE_NS + 5.0 for o, l, r in part)
-            add("T", cost, ("acc", part, first, last), [x for o, l, r in part for x in (l, r)] + [gate], [o for o, l, r in part])
-        return early[0][0]
+    def MM(groups):
+        add("T", sum(mcost(r) for o, ts in groups for l, r in ts), ("mm", groups), [x for o, ts in groups for t2 in ts for x in t2], [o for o, ts in groups])
+
+    def ACC(*parts):
+        parts = [p for p in parts if p]
+        for k, part in enumerate(parts):
+            add("T", sum(mcost(r) for o, l, r in part), ("acc", part, k == 0, k == len(parts) - 1), [x for o, l, r in part for x in (l, r)], [o for o, l, r in part])
+        return parts[0][0][0]
 
     def M1(ts, n=H):
         o = tile(n)
         MM([(o, ts)])
         return o
+
+    def M2(early, late):
+        o = tile(H)
+        return ACC([(o, l, r) for l, r in early], [(o, l, r) for l, r in late])
 
     def GATHER(eng, out, win, off, sub=None):
         add(eng, 60.0 + out["n"] * GR * CYC, ("gather", eng, out, win, off, sub), [win, off, sub], [out])
@@ -137,11 +141,12 @@ def build(PE_NS, CYC, LAT, RLAT, VFIX, SFIX, TT2, GR):
         lat = 2000.0 + 128 * v["n"] * WIDE[v["dt"]] / 180.0
         add("D", 60.0, (kind, v, name, a, b, sem), [v] if kind == "store" else [], [v] if kind == "load" else [], lat, sem)
 
-    def SEND(src, dst, hop):
+    def SEND(src, dst, hop, cap=None):
         sem = "r%d" % len(sems)
         sems.append(sem)
         lat = RLAT + 128 * src["n"] * WIDE[src["dt"]] / 70.0
-        j = add("G", 400.0, ("send", src, dst, hop, sem), [src], [], 0.0, "sent")
+        sems.append("s" + sem)
+        j = add("G", 400.0, ("send", src, dst, hop, sem, cap), [src, cap], [], 0.0, "s" + sem)
         k = add("R", 0.0, ("recv", hop), [], [dst], lat, sem)
         ops[k]["deps"].add(j)
 
@@ -149,15 +154,16 @@ def build(PE_NS, CYC, LAT, RLAT, VFIX, SFIX, TT2, GR):
     ps_in, dv_in, ex_in = buf("ps_in", I), buf("dv_in", I), buf("ex_in", 4 * I)
     nm_in, dn_in = buf("nm_in", I, "int32"), buf("dn_in", 4 * I, "int32")
     wt_in, th_in = buf("wt_in", 1, "int32"), buf("th_in", 1, "int32")
-    DMA("load", view(ex_in, 0, 2 * I), "ex", 0, 2 * I)
     DMA("load", ps_in, "ps", 0, I)
+    DMA("load", view(ex_in, 0, 2 * I), "ex", 0, 2 * I)
+    DMA("load", dv_in, "dv", 0, I)
     DMA("load", view(ex_in, 2 * I, 4 * I), "ex", 2 * I, 4 * I)
-    for v, name in ((dv_in, "dv"), (dn_in, "dn"), (nm_in, "nm")):
+    for v, name in ((dn_in, "dn"), (nm_in, "nm")):
         DMA("load", v, name, 0, v["n"])
-    DMA("load", view(X, X0, X0 + W), "xt", 0, W)
+    DMA("load", view(X, 0, W), "xt", 0, W)
     for v, name in ((wt_in, "wt"), (th_in, "th")):
         DMA("load", v, name, 0, 1)
-    SET(view(X, X0 + W, X0 + W + 16), 0.0)
+    SET(view(X, W, W + 16), 0.0)
 
     f32 = lambda name, n=1: buf(name, n, "float32")
     pi_ = IOTA(buf("p_i", 1, "int32"), [[0, 1]], 0, 1)
@@ -169,318 +175,345 @@ def build(PE_NS, CYC, LAT, RLAT, VFIX, SFIX, TT2, GR):
     ident = TS(buf("ident", 128), mdiff, 0.0, ALU.is_equal)
     blk = TS(buf("blk", 128), view(mgrp, 0, 128), gc, ALU.is_equal)
     ones = SET(buf("ones", 128), 1.0)
+    ones32 = IOTA(f32("ones32", 128), [[0, 128]], 1, 0)
+    zeros = SET(buf("zeros", 128), 0.0)
+    turn, late = [0], [False]
+
+    def DIAG(out, base, c):
+        add("G", 170.0 + 256 * CYC, ("diag", out, base, float(c)), [base], [out], alone=True)
+        return out
 
     def scaled(base, c, name):
         if c == 1.0:
             return base
         if name not in slots:
             turn[0] += 1
-            if late[0] and base is ident:
-                add("G", 170.0 + 256 * CYC, ("diag", buf(name, 128), zeros, c), [zeros], [slots[name]])
-            elif turn[0] % 3 == 0:
-                AC(buf(name, 128), base, ACT.Identity, scale=c)
+            if late[0] and base is ident and not isinstance(c, dict):
+                DIAG(buf(name, 128), zeros, c)
+            elif turn[0] % OPT["turn"]:
+                AC(buf(name, base["n"]), base, ACT.Identity, scale=c, alone=True)
             else:
-                TS(buf(name, 128), base, c, ALU.mult)
+                TS(buf(name, base["n"]), base, c, ALU.mult, alone=True)
         return slots[name]
-    turn, late = [0], [False]
-    zeros = SET(buf("zeros", 128), 0.0)
     sI = lambda c: scaled(ident, float(c), "I%g" % c)
     sB = lambda c: scaled(blk, float(c), "B%g" % c)
-    col = lambda name, a, b: TS(f32(name), kc, float(a), ALU.mult, float(b), ALU.add)
+    col = lambda name, a, b: AC(f32(name), kc, ACT.Identity, float(a), float(b))
+
+    def mix(name, i, b):
+        return DIAG(buf(name, 128), scaled(blk, b, name + "b") if isinstance(b, dict) else sB(b), i)
     k1, nk1 = col("k1", 1, 1), col("nk1", -1, -1)
-    Bk = scaled(blk, k1, "Bk")
-    Bkh = scaled(blk, col("k1h", 0.5, 0.5), "Bkh")
-    Bk16h = scaled(blk, col("k16", 0.5, -8), "Bk16h")
-    Dk15 = scaled(ident, col("k15", 1, -15), "Dk15")
     mv = view(mvar, 0, 128)
-    Bp = TT(buf("Bp", 128), TT(buf("c12", 128), TS(buf("c13", 128), mv, 8.0, ALU.mult, 1408.0, ALU.add), blk, ALU.mult), sI(256), ALU.add)
-    IH = TT(buf("IH", 128), ident, sB(0.5), ALU.subtract)
-    I7 = TT(buf("I7", 128), ident, sB(7), ALU.subtract) if DVA else None
-    IB = TT(buf("IB", 128), sI(512), sB(512), ALU.subtract) if NEXTP else None
-    Bqh = TT(buf("Bqh", 128), TS(buf("c0", 128), mv, 240.0, ALU.add), sB(0.5), ALU.mult)
+    IH = mix("IH", 0.5, -0.5)
+    tri = TT(buf("c20", 128), TS(buf("c21", 128), mdiff, 0.0, ALU.is_gt, -15.0 / 16, ALU.mult), TS(buf("c22", 128), ident, 17.0 / 16, ALU.mult, -1.0 / 16, ALU.add), ALU.add)
+    tri = TT(buf("c23", 128), tri, blk, ALU.mult)
+    big = SET(f32("big", 2), 2.0 ** 62)
+    Tri = TS(buf("Tri", 128), tri, 2.0 ** 62, ALU.mult, view(big, 0, 1), ALU.mult)
     T2 = TT(buf("T2", 128), TS(buf("c1", 128), mv, 0.0, ALU.is_equal, 8.0, ALU.add), blk, ALU.mult)
     near = TS(buf("c2", 128), AC(f32("c3", 128), mdiff, ACT.Abs), 1.0, ALU.is_equal)
     first8 = TS(f32("first8"), kc, 0.0, ALU.is_equal, -8.0, ALU.mult)
     T1 = TT(buf("T1", 128), TS(buf("c4", 128), TT(buf("c5", 128), near, sI(-2), ALU.add), first8, ALU.add), blk, ALU.mult)
     Z = TT(buf("Z", 144), TS(buf("c6", 144), mgrp, gc, ALU.is_equal), TS(buf("c7", 144), mvar, 15.0, ALU.is_equal), ALU.mult)
-    Wb = scaled(blk, CP(f32("wt"), wt_in), "Wb")
-    at = TS(buf("c8", 128), mv, kc, ALU.is_equal, 4.0, ALU.mult)
-    Mw = TT(buf("c9", 128), at, TS(buf("c10", 128), mv, k1, ALU.is_equal), ALU.subtract)
-    Mw = AC(f32("Mw", 128), Mw, ACT.Identity, 2.0 ** 19)
-    n15 = TS(f32("n15"), kc, 15.0, ALU.is_lt)
-    fixc = TS(f32("fixc"), n15, 2.0 ** 19, ALU.mult, -32.0, ALU.add)
-    c16 = TS(f32("c16", 8), IOTA(f32("c11", 8), [[16, 8]], 0, 0), kc, ALU.add, 16.0, ALU.mult)
-    Mneg = SET(buf("Mneg", 1024), 0.0)
-    SET(view(Mneg, 0, 1024, 16), -1024.0)
-    Mkey = SET(f32("Mkey", 512), 2.0 ** 20)
-    SET(view(Mkey, 0, 512, 4), HH)
-    fused = "F" in PATHS
-    if fused:
-        Mrun = SET(buf("Mrun", 1024), 1.0)
-        SET(view(Mrun, 0, 1024, 16), 0.0)
-        for h in range(2):
-            SET(buf("seed%d" % h, 2048), 0.0)
-    nth = TS(f32("nth"), th_in, -1.0, ALU.mult, -102.0, ALU.add)
+    into = lambda z, k: view(z, 15 - k, 143 - k)
+    if "V" in OPT["wraph"] + OPT["wrapc"]:
+        at = TS(buf("c8", 128), mv, kc, ALU.is_equal, 4.0, ALU.mult)
+        Mw = TT(buf("c9", 128), at, TS(buf("c10", 128), mv, k1, ALU.is_equal), ALU.subtract)
+        Mw = AC(f32("Mw", 128), Mw, ACT.Identity, 2.0 ** 19)
+        n15 = TS(f32("n15"), kc, 15.0, ALU.is_lt)
+        fixc = TS(f32("fixc"), n15, 2.0 ** 19, ALU.mult, -32.0, ALU.add)
+        fixs = TS(f32("fixs"), n15, -2.0 ** 19, ALU.mult, 65536.0, ALU.add)
+    Mkey = IOTA(f32("Mkey", 512), [[0, 128], [1, 4]], 0, 0)
+    AC(Mkey, Mkey, ACT.Identity, 2.0 ** 20)
+    Lp = mix("Lp", -50, -52)
+    Mj, Mf = mix("Mj", -32.5, col("k2h", -0.5, -1)), mix("Mf", -101, col("k2", -1, -2))
+    bb = col("bb", 0.5, -106.5)
+    Bk16h = scaled(blk, col("k16", 0.5, -8), "Bk16h")
+    IHk = [scaled(IH, CK[d] + 4096, "IH%d" % d) for d in range(4)]
+    I7k = [mix("I7%d" % d, -6 * CK[d] - 7 * 4096, -7 * CK[d] - 8 * 4096) for d in range(4)]
 
-    def top(out, Wt, on):
-        P = M1([(IH, Wt)])
-        if on == "S":
-            return AC(out, P, ACT.Sign, 1.0, TINY)
-        TS(out, P, 0.0, ALU.is_gt, -0.5, ALU.add)
-        return TS(out, out, 2.0, ALU.mult)
+    def top(out, Wt, acc=None):
+        return AC(out, M1([(IH, Wt)]), ACT.Sign, 1.0, TINY, acc)
 
     def slot(kind, t, h):
-        sz, sb = buf("%sz%d%d" % (kind, t, h), 4 * H), buf("%sb%d%d" % (kind, t, h), (3 + NEXTP) * H)
+        t = t if kind == "i" else t % 2
+        sz, sb = buf("%sz%d%d" % (kind, t, h), 4 * H), buf("%sb%d%d" % (kind, t, h), 4 * H)
         sf, so = buf("%sf%d%d" % (kind, t, h), 3 * H, "float16"), buf("%so%d%d" % (kind, t, h), H + 8, "uint16")
-        return {"sb": sb, "sf": sf, "so": so, "z": sz, "r": view(sb, 0, H), "u": view(sb, H, 2 * H), "D": view(sb, 2 * H, 3 * H), "q": view(sb, 3 * H, 4 * H), "dn": view(sf, 0, 2 * H),
+        return {"sb": sb, "sf": sf, "so": so, "z": sz, "r": view(sb, 0, H), "un": view(sb, H, 2 * H), "D": view(sb, 2 * H, 3 * H), "q": view(sb, 3 * H, 4 * H), "dn": view(sf, 0, 2 * H),
                 "dv": view(sf, 0, H), "nm": view(sf, H, 2 * H), "mc": view(sf, 2 * H, 3 * H), "off": view(so, 0, H), "offc": view(so, H, H + 8)}
     pl = lambda v, d: view(v, d * H, (d + 1) * H)
+    nat = lambda v, d: view(v, d, 4 * H, 4)
 
     dn_own, dn_nxt = buf("dn_own", 8 * H, "float16"), buf("dn_nxt", 8 * H, "float16")
     for h in range(2):
         TS(view(dn_own, 4 * H * h, 4 * H * (h + 1)), view(dn_in, 4 * H * h, 4 * H * (h + 1)), -2048.0, ALU.add)
     SEND(dn_own, dn_nxt, -1)
 
-    def held(name, dv, u):
-        x, out = TT(buf(name + "x", H), dv, u, ALU.subtract), buf(name, 4 * H)
-        for d in range(4):
-            TS(pl(out, d), x, 12.0 - d - 51.0, ALU.is_equal)
-        return out
-
-    def logic(t, h, r, z, S, dnc, pf, dA):
+    def logic(t, h, r, r2, z, a, pf, full, oc, S, dnc):
         b = lambda name, n=H, dt="bfloat16": buf("L%s%d%d" % (name, t % 2, h), n, dt)
-        if pf is None:
-            Wo = AC(b("Wo"), r, ACT.Exp, -LN2, 110 * LN2)
-            pf = TT(b("pf"), Wo, M1([(sB(0.5), Wo)]), ALU.is_gt)
-        if WMV:
-            Wy = AC(b("Wy"), r, ACT.Exp, LN2, -117 * LN2)
+        phase[:] = ["L%d%d" % (h, t > 0), 0]
         tt = b("t", 4 * H)
-        if PICK_ON == "V":
+        if OPT["pick"] == "V":
             for d in range(4):
                 TT(pl(tt, d), pl(z, d), pf, ALU.mult)
+        elif OPT["pick"] == "P":
+            PK = tile()
+            MM([(pl(PK, d), [(ident, pf)]) for d in range(4)])
+            TT(tt, PK, z, ALU.mult)
         else:
             PK = tile()
-            MM([(pl(PK, d), [(ident, pl(z, d)), (sI(32), pf)]) for d in range(4)])
-            AC(tt, PK, ACT.Relu, 1.0, -32.0)
-        full = TT(b("full"), pf, AC(b("on"), r, ACT.Relu, 1.0, 1.0), ALU.min)
+            ACC([(PK, ident, z)], [(pl(PK, d), sI(128), pf) for d in range(4)])
+            AC(tt, PK, ACT.Relu, 1.0, -128.0)
         R = b("R", 4 * H)
-        for j in range(RSPLIT):
-            w = 4 * H // RSPLIT
+        for j in range(OPT["rsplit"]):
+            w = 4 * H // OPT["rsplit"]
             AC(view(R, w * j, w * (j + 1)), M1([(blk, view(tt, w * j, w * (j + 1)))], w), ACT.Relu, 1.0, nk1)
-        G = tile(H)
-        ACC([(G, T2, pl(tt, d)) for d in range(4)] + [(G, sB(-64), full)], [(G, T1, pl(R, d)) for d in range(4)], tt)
-        if WMV:
-            Wm = TT(b("Wm"), TS(b("fl"), G, 33.0, ALU.is_ge), Wy, ALU.mult)
-        g1 = AC(b("g1"), G, ACT.Relu, -1.0, 33.0)
-        if not WMV:
-            Wm = AC(b("Wm"), M1([(ident, r), (sI(-512), g1)]), ACT.Exp, LN2, -117 * LN2)
-        jf = top(b("jf"), Wm, TOP_ON[0])
-        none = TS(b("none"), M1([(blk, g1), (sI(-64), pf)]), -48.0, ALU.is_equal)
-        dvm = TT(b("dvm"), S["dv"], jf, ALU.mult)
-        tg = b("tg", 4 * H)
-        for d in range(4):
-            TS(pl(tg, d), dvm, 12.0 - d, ALU.is_equal)
-        if dA is None or (NEXTP and t < NV - 1):
-            q = AC(S["q"] if NEXTP else b("q"), M1([(ident, pf), (IH, jf)]), ACT.Relu, 1.0, -7.0)
-        elif NEXTP:
-            AC(S["q"], pf, ACT.Identity)
+        G = M2([(T2, pl(tt, d)) for d in range(4)] + [(sB(-64), full)] + ([(Boc, oc)] if oc else []), [(T1, pl(R, d)) for d in range(4)])
+        g1 = AC(b("g1"), G, ACT.Relu, -1.0, -31.5 if oc else 33.0)
+        Wm = AC(b("Wm"), M2([(ident, r)], [(sI(-512), g1)]), ACT.Exp, LN2, -117 * LN2)
+        cnt = f32("cnt%d%d" % (t, h)) if t < NV - 1 else None
+        jf = top(b("jf"), Wm, cnt)
+        none = TS(b("none"), M1([(sI(-64), pf), (blk, g1)]), -48.0, ALU.is_equal)
+        q = AC(S["q"], M1([(ident, pf), (IH, jf)]), ACT.Relu, 0.5, -3.5)
         KP = tile()
-        nat = lambda v, d: view(v, d, 4 * H, 4)
-        early = [(KP, ident, dnc)] + [(nat(KP, d), sI(-65536), pl(z, d)) for d in range(4)]
-        if dA is None:
-            ACC(early, [x for d in range(4) for x in ((nat(KP, d), sI(CK[d]), q), (nat(KP, d), sI(-65536), pl(tg, d)))], g1)
-        else:
-            ACC(early + [x for d in range(4) for x in ((nat(KP, d), sI(-65536), pl(dA, d)), (nat(KP, d), scaled(I7, CK[d], "I7%d" % d), pf))],
-                [(nat(KP, d), scaled(IH, CK[d], "IH%d" % d), jf) for d in range(4)], R)
-        key = SCAN(b("key", 4 * H, "float32"), Mkey, KP, HH, ALU.min, ALU.max)
-        m = M1([(ident, nat(dnc, 0)), (sI(CK[0]), full), (sI(CK[0]), none)])
-        TT(m, m, view(key, 3, 4 * H, 4), ALU.max)
+        early = [(KP, ident, dnc)] + [(nat(KP, d), sI(-65536), pl(a, d)) for d in range(4)] + [(nat(KP, 0), sI(6553600), full)]
+        ACC(early + [(nat(KP, d), I7k[d], pf) for d in range(4)], [(nat(KP, 0), sI(17 * 65536), none)] + [(nat(KP, d), IHk[d], jf) for d in range(4)])
+        m = nat(SCAN(tile(), Mkey, KP, 0.0, ALU.min, ALU.max), 3)
         late[0] = True
-        big = 1.5 * 2.0 ** 36
-        TS(S["D"], m, big, ALU.add, -big, ALU.add)
+        rnd = 1.5 * 2.0 ** 36
+        TS(S["D"], m, rnd, ALU.add, -rnd, ALU.add)
         TT(S["mc"], m, S["D"], ALU.subtract)
         RR = tile(2 * H)
-        MM([(pl(RR, 0), [(sI(119), ones), (sI(-256), full), (Dk15, full), (sI(-136), jf)]),
-            (pl(RR, 1), [(Bp, pf), (Bqh, jf)])])
-        TT(S["r"], pl(RR, 1), TT(b("r1"), pl(RR, 0), r, ALU.min), ALU.max)
-        TS(S["u"], S["r"], -4096.0, ALU.mult, 51.0, ALU.max)
-        CL = tile(2 * H)
-        cP, LP = pl(CL, 0), pl(CL, 1)
-        MM([(cP, [(sI(2080), ones), (blk, S["mc"])]), (LP, [(sI(4096), S["u"]), (sB(101), S["mc"])])])
+        MM([(pl(RR, 0), [(sB(95), pf), (sI(-320), full), (sI(-161), jf)]), (pl(RR, 1), [(Lp, pf), (blk, jf)])])
+        TT(S["r"], pl(RR, 1), TT(b("r1"), pl(RR, 0), r2, ALU.min), ALU.max)
+        TS(S["un"], S["r"], 0.0, ALU.is_lt)
+        cP = M2([(sB(2080), pf)], [(blk, S["mc"])])
+        LP = M2([(sB(208896), pf), (sI(2 ** 23), S["un"])], [(sB(101), S["mc"])])
         e = TT(b("e", H, "int32"), cP, S["nm"], ALU.mult)
         TS(e, e, 5, ALU.arith_shift_right, 4095, ALU.bitwise_and)
         TT(e, LP, e, ALU.add)
-        sc = SCAN(b("sc", H, "float32"), Mw, cP, 0.0, ALU.add, ALU.min)
-        TS(e, e, 0x7F800FFF, ALU.bitwise_and)
+        TS(e, e, 0x800FFF, ALU.bitwise_and)
         TS(S["off"], e, float(ZCOL), ALU.min)
-        TS(S["offc"], view(sc, 15, H, 16), fixc, ALU.add)
+        if OPT["wrapc"] == "V":
+            sc = SCAN(b("sc", H, "float32"), Mw, cP, 0.0, ALU.add, ALU.min)
+            TS(S["offc"], view(sc, 15, H, 16), fixc, ALU.add)
+        else:
+            TS(S["offc"], M1([(into(Z, k), view(S["mc"], k, H, 16)) for k in range(16)], 8), 2048.0, ALU.add)
         if t > 0:
             for k in ("so", "sb", "sf"):
                 SEND(S[k], slot("i", t, h)[k], 1)
         W2 = AC(b("W2"), M1([(ident, r), (sI(-512), g1), (sI(-256), jf)]), ACT.Exp, LN2, -373 * LN2)
-        j2 = top(b("j2"), W2, TOP_ON[1])
-        keep = b("keep", 4 * H)
-        if REL_ON == "V":
-            RP = M1([(sI(68), ones), (Bkh, jf), (Bk, full), (sI(17), none)])
-            for d in range(4):
-                TT(pl(keep, d), RP, pl(z, d), ALU.not_equal)
+        j2 = top(b("j2"), W2)
+        x = AC(b("x"), M1([(sI(16), jf), (Bk16h, j2)]), ACT.Relu, 1.0, -67.0)
+        DF = tile()
+        if OPT["b"] == "V":
+            sh = TS(b("b", H, "float16"), M1([(Mj, jf), (Mf, full), (sI(-18), none), (sI(1 / 32), x)]), bb, ALU.add)
+            ACC([(DF, ident, a)], [(pl(DF, d), ident, sh) for d in range(4)])
         else:
-            rel = AC(b("rel"), M1([(Bkh, jf), (Bk, full), (sI(17), none)]), ACT.Identity, 1.0, 68.0)
-            DF = tile()
-            ACC([(DF, ident, z)], [(pl(DF, d), sI(-1), rel) for d in range(4)])
-            AC(keep, DF, ACT.Abs, 32.0)
-        ZA = tile()
-        ACC([(ZA, ident, z), (ZA, sI(-64), tg)], [(pl(ZA, d), sI(-64), full) for d in range(4)])
-        TT(keep, ZA, keep, ALU.mult if REL_ON == "V" else ALU.min)
-        a2 = AC(b("a2"), M1([(sI(32), full), (sB(8.5), jf), (Bk16h, j2)]), ACT.Identity, 1.0, 36.0)
-        U2 = tile()
-        ACC([(U2, sI(32), tg)], [(pl(U2, d), ident, a2) for d in range(4)])
-        TT(S["z"], U2, keep, ALU.max)
+            sh = AC(b("b"), M1([(Mj, jf), (Mf, full), (sI(-18), none)]), ACT.Identity, 1.0, bb)
+            ACC([(DF, ident, a)] + [(pl(DF, d), ident, sh) for d in range(4)], [(pl(DF, d), sI(1 / 32), x) for d in range(4)])
         if t > 0:
-            SEND(S["z"], slot("i", t, h)["z"], 1)
-        if t < NV - 1:
-            AC(b("junk"), M1([(ones, jf)]), ACT.Identity, 0.5, 64.0, acc=f32("cnt%d%d" % (t, h)))
-            if h == 1:
-                n = TT(buf("cn%d" % t, 1, "int32"), f32("cnt%d0" % t), f32("cnt%d1" % t), ALU.add)
-                TS(n, n, 7, ALU.bitwise_and)
-                SEND(TS(f32("ao%d" % t), n, -32.0, ALU.mult), f32("ai%d" % (t + 1)), 2 if t > 0 else 1)
+            SEND(a, slot("i", t, h)["z"], 1, AC(S["z"], DF, ACT.Abs, 32.0))
+        else:
+            TT(S["z"], AC(DF, DF, ACT.Abs, 32.0), a, ALU.min)
+        if t < NV - 1 and h == 1:
+            n = TS(buf("cn%d" % t, 1, "int32"), M1([(ones32, f32("cnt%d0" % t)), (ones32, cnt)], 1), 0.5, ALU.mult, 16384.0, ALU.add)
+            TS(n, n, 7, ALU.bitwise_and)
+            SEND(TS(f32("ao%d" % t), n, -32.0, ALU.mult), f32("ai%d" % (t + 1)), 2 if t > 0 else 1)
 
     def reads(t, h, S, thA):
         b = lambda name, n=H, dt="bfloat16": buf("G%s%d" % (name, h), n, dt)
-        win = view(X, X0, X0 + W + 16)
-        xc = view(slots["seed%d" % h], 0, 2048, 16) if fused else b("xc")
-        GATHER(XC_ON, xc, win, S["offc"])
+        phase[:] = ["G%d" % h, 0]
+        win = view(X, 0, W + 16)
+        fused = "F" in paths[2 * h:2 * h + 2]
+        xc = view(seeds[h], 0, 2048, 16) if fused else b("xc")
+        GATHER(OPT["xc"], xc, win, S["offc"])
         SP, y, ad, ym = tile(H), b("y", 2048), b("ad", 2048), b("ym", 2048)
         for c in range(2):
-            path = PATHS[2 * h + c]
+            path = paths[2 * h + c]
             yc, ac, xcc, off = view(y, 1024 * c, 1024 * (c + 1)), view(ad, 1024 * c, 1024 * (c + 1)), view(xc, 64 * c, 64 * (c + 1)), view(S["off"], 64 * c, 64 * (c + 1))
-            n = 1024 // GSPLIT
+            gs = OPT["gsplit"]
+            n = 1024 // gs
             part = lambda v, j, w: view(v, w * j, w * (j + 1))
             if path == "F":
-                rep = SCAN(buf("rep%d%d" % (h, c), 1024), Mrun, view(slots["seed%d" % h], 1024 * c, 1024 * (c + 1)), 0.0, ALU.mult, ALU.add)
-                for j in range(GSPLIT):
+                rep = SCAN(buf("rep%d%d" % (h, c), 1024), Mrun, view(seeds[h], 1024 * c, 1024 * (c + 1)), 0.0, ALU.min, ALU.max)
+                for j in range(gs):
                     GATHER("V", part(yc, j, n), win, part(off, j, n // 16), part(rep, j, n))
                     AC(part(ac, j, n), part(yc, j, n), ACT.Abs)
                 lanes = [view(ac, k, 1024, 16) for k in range(16)]
             else:
-                for j in range(GSPLIT):
+                for j in range(gs):
                     GATHER(path, part(yc, j, n), win, part(off, j, n // 16))
                 for half in range(2):
                     DP = tile()
                     MM([(part(DP, j, 64), [(ident, view(yc, 8 * half + j, 1024, 16)), (sI(-1), xcc)]) for j in range(8)])
                     AC(part(ac, half, 512), DP, ACT.Abs)
                 lanes = [part(ac, k, 64) for k in range(16)]
-            MM([(part(SP, c, 64), [(sI(2), part(S["u"], c, 64))] + [(view(Z, 15 - k, 143 - k), lanes[k]) for k in range(16)])])
-            SCAN(part(ym, c, 1024), Mneg, yc, -1024.0, ALU.add, ALU.max)
-        nc = TS(b("nc"), SP, thA, ALU.add, 0.0, ALU.is_le) if CLV else AC(b("nc"), SP, ACT.Relu, 1.0, thA)
-        return xc, view(ym, 15, 2048, 16), nc
+            MM([(part(SP, c, 64), [(sI(8192), part(S["un"], c, 64))] + [(into(Z, k), lanes[k]) for k in range(16)])])
+            SCAN(part(ym, c, 1024), Mrun, yc, 0.0, ALU.min, ALU.max)
+        if OPT["wc"] == "V":
+            cf = TS(b("cf"), SP, thA, ALU.add, 0.0, ALU.is_le)
+        else:
+            cf = AC(b("cf"), AC(SP, SP, ACT.Sign, -1.0, thA), ACT.Relu)
+        return xc, view(ym, 15, 2048, 16), cf
 
     def update(t, h, S, got, N_):
-        xc, Y, nc = got
+        xc, Y, cf = got
         b = lambda name, n=H, dt="bfloat16": buf("U%s%d%d" % (name, t % 2, h), n, dt)
-        r = S["r"]
-        Wy = AC(b("Wy"), M1([(ident, r), (sI(-1), S["u"])]), ACT.Exp, LN2, -66 * LN2)
-        npv = AC(b("np"), M1([(ident, r), (sI(256), top(b("ny"), Wy, TOP_ON[2]))]), ACT.Relu, 1.0, -255.0)
+        last = t == NV - 1
+        phase[:] = ["U%d%d" % (h, last), 0]
+        r, un, q, z = S["r"], S["un"], S["q"], S["z"]
+        npv = AC(b("np"), M1([(ident, r), (sI(256), top(b("ny"), AC(b("Wy"), r, ACT.Exp, LN2, -117 * LN2)))]), ACT.Relu, 1.0, -255.0)
         pen = b("pen", 4 * H)
+        c0, c1 = (67.0 / 32, -32) if last else (95.0 / 32, -128)
         for d in range(4):
-            TS(pl(pen, d), S["D"], CK[d], ALU.not_equal, -2.125, ALU.add)
-        hasn = TS(b("hasn"), S["D"], HH, ALU.is_equal, 8.0, ALU.add)
-        has0 = AC(b("has0"), hasn, ACT.Identity, 1.0, -8.9375)
-        X1 = tile(H)
-        ahead = NEXTP and t < NV - 1
-        early = [(X1, ident, r), (X1, ident, S["u"])] + ([(X1, sB(512), has0)] if ahead else [])
-        if CLV:
-            Wc = TT(b("Wc"), AC(b("Wo"), ACC(early, []), ACT.Exp, -LN2, 174 * LN2), nc, ALU.mult)
+            TS(pl(pen, d), S["D"], CK[d], ALU.not_equal, -c0 if last else c0, ALU.add)
+        hn = TT(b("hn"), q, S["D"], ALU.is_gt)
+        Wo = AC(b("Wo"), M1([(ident, r), (sI(512), un), (sB(512), hn)]), ACT.Exp, -LN2, 120 * LN2)
+        oc = top(b("oc"), TT(b("Wc"), Wo, cf, ALU.mult))
+        cnt = M2([(blk, hn)], [(blk, cf)])
+        nokb = AC(b("nokb"), cnt, ACT.Sign) if OPT["nokb"] == "S" else TS(b("nokb"), cnt, 0.5, ALU.is_gt)
+        pf = full = None
+        if not last:
+            pA = AC(b("pA"), M1([(Tri, un), (Tq, q), (IH, Wo)]), ACT.Sign, 1.0, TINY)
+            if OPT["pfs"]:
+                pf = TT(b("pf"), nokb, AC(b("s"), M1([(sI(-2), q), (sI(-1), pA)]), ACT.Identity, 1.0, 1.0), ALU.is_equal)
+            else:
+                pf = TS(b("pf"), M2([(sI(2), q), (ident, pA)], [(ident, nokb)]), 1.0, ALU.is_equal)
+            full = TT(b("full"), pf, un, ALU.is_gt) if OPT["full"] == "V" else AC(b("full"), M2([(sI(-1), un)], [(ident, pf)]), ACT.Relu)
+        if OPT["nok"] == "V":
+            nok = TT(b("nok"), nokb, q, ALU.is_ge)
         else:
-            Wc = AC(b("Wc"), ACC(early, [(X1, sI(512), nc)], Y), ACT.Exp, -LN2, 174 * LN2)
-        oc = top(b("oc"), Wc, TOP_ON[3])
-        dA = held("UdA%d%d" % (t % 2, h), S["dv"], S["u"]) if DVA and t < NV - 1 else None
-        pf = None
-        if ahead:
-            rA = TT(b("rA"), M1([(blk, npv), (IB, S["q"])]), r, ALU.max)
-            WA = AC(b("WA"), rA, ACT.Exp, -LN2, 110 * LN2)
-            pA = TT(b("pA"), WA, M1([(sB(0.5), WA)]), ALU.is_gt)
-            PF = tile(H)
-            pf = TS(b("pf"), ACC([(PF, ident, S["q"]), (PF, sI(-1), pA), (PF, sB(-2), hasn)], [(PF, sB(-1), oc)], Wc), -271.0, ALU.is_equal)
-        RU = tile(H)
-        r2 = TT(b("r"), ACC([(RU, blk, npv), (RU, sI(-512), hasn)], [(RU, sB(-256), oc)], Wc), r, ALU.max)
+            nok = AC(b("nok"), M2([(sI(-2), q)], [(ident, nokb)]), ACT.Identity, 1.0, 1.0)
+        r2 = TT(b("r"), M2([(blk, npv)], [(sI(-512), nok)]), r, ALU.max)
         U5 = tile()
-        ACC([(U5, sI(-32), pen)], [(pl(U5, d), Bkh, oc) for d in range(4)], Wc)
-        z2 = TT(b("z", 4 * H), U5, S["z"], ALU.max)
-        CLP = tile()
-        nok = AC(b("nok"), M1([(ident, hasn), (sB(0.5), oc)]), ACT.Identity)
-        MM([(pl(CLP, 0), [(sI(1 / 8192), S["D"]), (sI(-16), nok)]), (pl(CLP, 1), [(ident, S["mc"]), (sI(-8192), nok)]),
-            (pl(CLP, 2), [(sI(1 / 8192), S["D"]), (sI(16), nok)]), (pl(CLP, 3), [(ident, S["mc"]), (sI(8192), nok)])])
-        TT(N_["dn"], view(CLP, 2 * H, 4 * H), TT(b("n1", 2 * H, "float16"), view(CLP, 0, 2 * H), S["dn"], ALU.max), ALU.min)
+        if last:
+            er = TS(b("er"), M1([(ident, S["dv"]), (sI(32), un)]), 0.0, ALU.is_gt)
+            zs = view(zs_in, H * h, H * (h + 1))
+            bit = TT(b("bx", H, "float32"), M1([(Bpow, er), (sB(2), q)]), AC(b("pw"), zs, ACT.Exp, -LN2), ALU.mult)
+            bit = TS(b("bit", H, "int32"), bit, -0.5, ALU.add)
+            gone = TT(b("gone"), TS(bit, bit, 1, ALU.bitwise_and), er, ALU.add)
+            zf = TS(b("zf"), M1([(ident, zs), (sI(-32), gone)]), 0.0, ALU.max, 128.0, ALU.add)
+            ZR = tile()
+            ACC([(ZR, sI(-2), z)], [(pl(ZR, d), ident, zf) for d in range(4)])
+            zr = TT(b("zr", 4 * H), ZR, z, ALU.min)
+            zb = AC(b("zb", 4 * H), zr, ACT.Relu, 18.0, -288.0)
+            ZP = tile()
+            MM([(nat(ZP, d), [(ident, pl(zr, d)), (sI(-1), pl(zb, d))]) for d in range(4)])
+            exr = AC(b("exr", 4 * H), ZP, ACT.Identity, 1.0, -1.0)
+            MM([(nat(U5, d), [(sI(c1), pl(pen, d)), (Bkh, oc)]) for d in range(4)])
+            a = TT(view(yg, 4 * H * h, 4 * H * (h + 1)), U5, exr, ALU.max)
+            TT(S["dv"], TS(b("dw", H, "float16"), S["dv"], 0.0, ALU.is_lt, 16.0, ALU.mult), S["dv"], ALU.add)
+        else:
+            ACC([(U5, sI(c1), pen)], [(pl(U5, d), Bv, oc) for d in range(4)], [(pl(U5, d), sI(164), full) for d in range(4)])
+            a = TT(b("a", 4 * H), U5, z, ALU.max)
+        if OPT["nm"] == "V":
+            CLP = tile()
+            MM([(pl(CLP, 0), [(sI(1 / 8192), S["D"]), (sI(-32), nok)]), (pl(CLP, 1), [(ident, S["mc"]), (sI(-8192), nok)]),
+                (pl(CLP, 2), [(sI(1 / 8192), S["D"]), (sI(32), nok)]), (pl(CLP, 3), [(ident, S["mc"]), (sI(8192), nok)])])
+            TT(N_["dn"], view(CLP, 2 * H, 4 * H), TT(b("n1", 2 * H, "float16"), view(CLP, 0, 2 * H), S["dn"], ALU.max), ALU.min)
+        else:
+            df, CLP = b("df", 2 * H, "float16"), tile(2 * H)
+            MM([(pl(CLP, 0), [(sI(1 / 8192), S["D"]), (sI(-1), S["dv"])]), (pl(CLP, 1), [(ident, S["mc"]), (sI(-1), S["nm"])])])
         HV = tile(2 * H)
         groups = []
         for c in range(2):
             s = lambda v: view(v, 64 * c, 64 * (c + 1))
-            f = PATHS[2 * h + c] == "F"
+            f = paths[2 * h + c] == "F"
             groups.append((s(pl(HV, 1)), [(sI(-0.25), s(ones)), (sI(1 if f else 0.5), s(xc)), (sI(0.5), s(Y))]))
-            groups.append((s(pl(HV, 0)), ([(Wb, s(xc))] if f else []) + [(Wb, s(Y))]))
+            if OPT["wraph"] == "V":
+                groups.append((s(pl(HV, 0)), ([(Wb, s(xc))] if f else []) + [(Wb, s(Y))] + ([(sI(65536), s(nokb))] if OPT["spare"] == 2 else [])))
+            else:
+                groups.append((view(HV, 4 * c, 4 * c + 4), [(into(Zw, k), view(s(v), k, 64, 16)) for k in range(16) for v in ([xc, Y] if f else [Y])]))
         MM(groups)
-        sh = SCAN(b("sh", H, "float32"), Mw, pl(HV, 0), 0.0, ALU.add, ALU.min)
-        big = 1.5 * 2.0 ** 23
-        if NV_ON == "V":
-            nv = TS(b("nv"), pl(HV, 1), big, ALU.add, -big, ALU.add)
+        sh = view(SCAN(b("sh", H, "float32"), Mw, pl(HV, 0), 0.0, ALU.add, ALU.min), 15, H, 16) if OPT["wraph"] == "V" else view(HV, 0, 8)
+        rnd = 1.5 * 2.0 ** 23
+        if OPT["nv"] == "V":
+            nv = TS(b("nv"), pl(HV, 1), rnd, ALU.add, -rnd, ALU.add)
         else:
-            nv = AC(b("nv"), AC(b("nw", H, "float32"), pl(HV, 1), ACT.Identity, 1.0, big), ACT.Identity, 1.0, -big)
-        hi = CP(b("hi", 8, "int32"), view(sh, 15, H, 16))
+            nv = AC(b("nv"), AC(b("nw", H, "float32"), pl(HV, 1), ACT.Identity, 1.0, rnd), ACT.Identity, 1.0, -rnd)
+        hi = CP(b("hi", 8, "int32"), sh)
         TS(hi, hi, 15, ALU.bitwise_and)
-        offs = CP(b("so", 8, "uint16"), TT(hi, c16, hi, ALU.add))
-        val = GATHER(XC_ON, b("old"), view(X, W // 2 * h, W // 2 * (h + 1)), offs)
-        for sign, o in ((-1, ALU.max), (1, ALU.min)):
-            P = tile(H)
-            ACC([(P, ident, nv), (P, sB(256 * sign), has0)], [(P, sB(256 * sign), nc)], nv)
-            val = TT(b("val%d" % sign), P, val, o)
-        return r2, z2, pf, dA, offs, val
-
-    def scatter(h, offs, nv):
-        win = view(X, W // 2 * h, W // 2 * (h + 1))
+        if OPT["spare"] == 2:
+            base = TT(b("base", 8, "float32"), TS(b("fl", 8, "float32"), sh, fixs, ALU.is_ge, float(SPARE), ALU.mult), view(c16, 0, 8), ALU.add)
+            offs = CP(b("so", 8, "uint16"), TT(hi, base, hi, ALU.add))
+            win = view(X, W // 2 * h, W // 2 * (h + 1) + SPARE)
+        elif OPT["spare"]:
+            base = tile(8)
+            ACC([(base, ident, c16h)], [(base, into(Zs, k), view(nokb, k, H, 16)) for k in range(16)])
+            offs = CP(b("so", 8, "uint16"), TT(hi, base, hi, ALU.add))
+            win = view(X, W // 2 * h, W // 2 * (h + 1) + SPARE)
+        else:
+            offs = CP(b("so", 8, "uint16"), TT(hi, view(c16, 0, 8), hi, ALU.add))
+            win = view(X, W // 2 * h, W // 2 * (h + 1))
+            val = GATHER(OPT["xc"], b("old"), win, offs)
+            for sign, o in ((-1, ALU.max), (1, ALU.min)):
+                val = TT(b("val%d" % sign), M2([(ident, nv)], [(sI(256 * sign), nokb)]), val, o)
+            nv = val
         add("V", 60.0 + H * 3.8 * CYC, ("scatter", win, offs, nv), [offs, nv], [win])
+        return r2, a, pf, full, oc
 
-    k16n = col("k16n", -1, 16)
+    zs_own, zs_in = buf("zs_own", I), buf("zs_in", I)
     for h in range(2):
         S = slot("i", 0, h)
-        p = view(ps_in, H * h, H * (h + 1))
-        r0 = TT(buf("r0%d" % h, H), TS(buf("r00%d" % h, H), p, k16n, ALU.mult), p, ALU.min)
-        z0, za, zb = buf("z0%d" % h, 4 * H), buf("za%d" % h, 4 * H), buf("zb%d" % h, 4 * H)
+        b = lambda name, n=H, dt="bfloat16": buf("P%s%d" % (name, h), n, dt)
+        p, dv = view(ps_in, H * h, H * (h + 1)), view(dv_in, H * h, H * (h + 1))
+        r0 = TT(b("r0"), TS(b("r00"), p, 64.0, ALU.mult), p, ALU.min)
+        un = TS(b("un"), p, 0.0, ALU.is_lt)
+        Wo = AC(b("Wo"), M1([(ident, p), (sI(512), un)]), ACT.Exp, -LN2, 120 * LN2)
+        pf = TS(b("pf"), M1([(Tri, un), (IH, Wo)]), 0.0, ALU.is_gt)
+        full = TT(b("full"), pf, un, ALU.is_gt)
         e = view(ex_in, 4 * H * h, 4 * H * (h + 1))
-        AC(zb, e, ACT.Relu, -18.0, -18.0)
+        zb = AC(b("zb", 4 * H), e, ACT.Relu, -18.0, -18.0)
         ZP = tile()
-        MM([(pl(ZP, d), [(ident, view(e, d, 4 * H, 4)), (ident, view(zb, d, 4 * H, 4))]) for d in range(4)])
-        AC(z0, ZP, ACT.Identity, 1.0, 1.0)
-        TS(S["dv"], view(dv_in, H * h, H * (h + 1)), -1.0, ALU.mult, 12.0, ALU.add)
+        MM([(pl(ZP, d), [(ident, nat(e, d)), (ident, nat(zb, d))]) for d in range(4)])
+        z0 = AC(b("z0", 4 * H), ZP, ACT.Identity, 1.0, 1.0)
+        x, held = TT(b("x"), TS(b("x0"), un, 8.0, ALU.mult), dv, ALU.add), b("held", 4 * H)
+        for d in range(4):
+            TS(pl(held, d), x, float(d), ALU.is_equal, HELD, ALU.mult)
+        FP = tile()
+        ACC([(FP, ident, held)], [(pl(FP, d), sI(100), full) for d in range(4)])
+        a = TT(b("a", 4 * H), TS(FP, FP, 100.0, ALU.min), z0, ALU.max)
+        TS(S["dv"], dv, -1.0, ALU.mult, -12.0, ALU.add)
         TS(S["nm"], view(nm_in, H * h, H * (h + 1)), -2048.0, ALU.add)
-        logic(0, h, r0, z0, S, view(dn_own, 4 * H * h, 4 * H * (h + 1)), None, None)
+        logic(0, h, r0, r0, z0, a, pf, full, None, S, view(dn_own, 4 * H * h, 4 * H * (h + 1)))
+        phase[0] = None
+        zx = TT(held, held, z0, ALU.min)
+        AC(view(zs_own, H * h, H * (h + 1)), M1([(ident, pl(zx, d)) for d in range(4)]), ACT.Identity)
+    SEND(zs_own, zs_in, NV - 1)
+
+    Tq = scaled(Tri, -2.0, "Tq")
+    Boc = mix("Boc", 4.5, 4)
+    Bv, Bkh = scaled(blk, col("k63", 0.5, -31.5), "Bv"), scaled(blk, col("k1h", 0.5, 0.5), "Bkh")
+    Bpow = scaled(blk, CP(f32("pw2"), AC(buf("pw1", 1), k1, ACT.Exp, LN2)), "Bpow")
+    wt = CP(f32("wt"), wt_in)
+    Wb, Zw = (scaled(blk, wt, "Wb"), None) if OPT["wraph"] == "V" else (None, scaled(Z, wt, "Zw"))
+    c16 = TS(f32("c16", 16), IOTA(f32("c11", 16), [[16, 16]], 0, 0), kc, ALU.add, 16.0, ALU.mult)
+    if OPT["spare"] == 1:
+        Zs, c16h = scaled(Z, SPARE / 16.0, "Zs"), CP(buf("c16h", 8, "float16"), view(c16, 0, 8))
+    Mrun = IOTA(buf("Mrun", 1024), [[0, 64], [2048, 16]], -1024, 0)
+    seeds = [buf("seed%d" % h, 2048) for h in range(2)]
+    for c in range(4):
+        if paths[c] == "F":
+            IOTA(view(seeds[c // 2], 1024 * (c % 2), 1024 * (c % 2 + 1)), [[0, 1024]], 0, 0)
+    nth = TS(f32("nth"), th_in, -1.0, ALU.mult)
 
     yn, yp, yd, yg = f32("yn_s", I), buf("yp_s", I), buf("yd_s", I), buf("yg_s", 4 * I)
     for t in range(NV):
+        phase[:] = ["A", 0]
         thA = nth if t == 0 else TS(f32("thA%d" % t), f32("ai%d" % t), nth, ALU.add)
-        got = []
+        got = [reads(t, h, slot("i", t, h), thA) for h in range(2)]
         for h in range(2):
-            first = len(ops)
-            got.append(reads(t, h, slot("i", t, h), thA))
-            for j, o in enumerate(x for x in ops[first:] if x["call"][0] == "gather" and PERIOD):
-                o["due"] = (NV - 1 - t) * PERIOD + (1 - h) * LEAD + REST - 500.0 * j
-        for h in range(2):
-            N_ = slot("o", t + 1, h)
-            r2, z2, pf, dA, offs, nv = update(t, h, slot("i", t, h), got[h], N_)
-            scatter(h, offs, nv)
+            N_, S = slot("o", t + 1, h), slot("i", t, h)
+            r2, a, pf, full, oc = update(t, h, S, got[h], N_)
             if t < NV - 1:
-                logic(t + 1, h, r2, z2, N_, view(dn_nxt, 4 * H * h, 4 * H * (h + 1)), pf, dA)
+                logic(t + 1, h, S["r"], r2, S["z"], a, pf, full, oc, N_, view(dn_nxt, 4 * H * h, 4 * H * (h + 1)))
             else:
+                phase[0] = None
                 s = lambda v: view(v, H * h, H * (h + 1))
-                DMA("store", view(X, X0 + W // 2 * h, X0 + W // 2 * (h + 1)), "yx", W // 2 * h, W // 2 * (h + 1))
+                DMA("store", view(X, W // 2 * h, W // 2 * (h + 1)), "yx", W // 2 * h, W // 2 * (h + 1))
                 TS(s(yn), N_["nm"], 2048.0, ALU.add)
-                TS(s(yd), N_["dv"], -1.0, ALU.mult, 12.0, ALU.add)
-                TT(s(yp), TS(buf("o1%d" % h, H), r2, -1.0, ALU.max), AC(buf("o2%d" % h, H), r2, ACT.Identity, 1.0, 15.0), ALU.min)
-                zb = AC(slots["zb%d" % h], z2, ACT.Relu, 18.0, -288.0)
-                ZP = tile()
-                MM([(view(ZP, d, 4 * H, 4), [(ident, pl(z2, d)), (sI(-1), pl(zb, d))]) for d in range(4)])
-                og = AC(view(yg, 4 * H * h, 4 * H * (h + 1)), ZP, ACT.Identity, 1.0, -1.0)
-                DMA("store", og, "yg", 4 * H * h, 4 * H * (h + 1))
+                TS(s(yd), N_["dv"], -1.0, ALU.mult, 4.0, ALU.add)
+                TT(s(yp), TS(buf("o1%d" % h, H), r2, -1.0, ALU.max), AC(buf("o2%d" % h, H), r2, ACT.Identity, 1.0, 64.0), ALU.min)
+                DMA("store", a, "yg", 4 * H * h, 4 * H * (h + 1))
                 ops[-1]["tail"] = LEAD * (1 - h)
     for v, name in ((yn, "yn"), (yp, "yp"), (yd, "yd")):
         DMA("store", v, name, 0, I)
@@ -497,14 +530,12 @@ def schedule(ops, tiles, costs):
             succ[d].append(j)
     users = [sorted({a[0] for a in t["acc"]}) for t in tiles]
     cost, lat = costs[0]
+    kin = [o["kin"] for o in ops]
 
     def run(off):
         prio = [0.0] * n
         for j in range(n - 1, -1, -1):
-            if "due" in ops[j]:
-                prio[j] = ops[j]["due"] + off.get(kin[j], 0.0)
-            else:
-                prio[j] = cost[j] + lat[j] + off.get(kin[j], 0.0) + max([prio[s] for s in succ[j]] + [ops[j].get("tail", 0.0)])
+            prio[j] = cost[j] + lat[j] + off.get(kin[j], 0.0) + max([prio[s] for s in succ[j]] + [ops[j].get("tail", 0.0)])
         left, ready = [len(p) for p in pred], [0.0] * n
         pool = {e: [j for j in range(n) if not left[j] and eng[j] == e] for e in "VSTGDR"}
         free = {e: 0.0 for e in pool}
@@ -560,12 +591,12 @@ def schedule(ops, tiles, costs):
             fin[j] = at + c[j] + l[j]
         return fin
 
-    sc = [j for j in range(n) if ops[j]["call"][0] == "scatter"]
-    per = sc[4] - sc[2]
-    kin = [j if j < sc[0] or j >= sc[0] + 5 * per else sc[0] + (j - sc[0]) % per for j in range(n)]
     kinds = sorted(set(kin))
     rng = np.random.default_rng(SEED)
     off, plan = {}, run({})
+    while plan is None:
+        off = {k: float(rng.normal()) * 300.0 for k in kinds}
+        plan = run(off)
     base = [max(length(plan[0], plan[1], c, l)) for c, l in costs]
     best = float(len(costs))
     now = best
@@ -612,7 +643,7 @@ def rank_program(g, core, T, topo):
             return t[:, v["lo"]:v["lo"] + v["n"]]
         return t[:, v["lo"]:v["lo"] + (v["n"] - 1) * v["st"] + 1:v["st"]]
 
-    mark, sent = {}, 0
+    mark = {}
     for e in ORDER:
         k = 0
         for j in ORDER[e]:
@@ -624,6 +655,8 @@ def rank_program(g, core, T, topo):
             elif o["sem"] is None:
                 k += 1
                 mark[j] = (counter[e], k)
+            else:
+                mark[j] = (o["sem"], len(topo.engines(core, cores[(rank + o["call"][3]) % len(cores)])))
 
     def emit(q, c):
         kind = c[0]
@@ -677,19 +710,23 @@ def rank_program(g, core, T, topo):
             for d in o["deps"]:
                 s, v = mark[d]
                 need[s] = max(need.get(s, 0), v)
+            c = o["call"]
             for s in sorted(need):
                 if need[s] > seen.get(s, 0):
                     q.wait_ge(T.sem[s], need[s])
                     seen[s] = need[s]
-            c = o["call"]
             if c[0] == "send":
                 dst = cores[(rank + c[3]) % len(cores)]
                 rid, pid, _ = topo.addr(dst)
-                q.remote_dma(ap(c[2]), ap(c[1]), T.sem[c[4]], T.sem["sent"], pid, rid, topo.mask(core, dst))
-                sent += len(topo.engines(core, dst))
+                if c[5] is None:
+                    q.remote_dma(ap(c[2]), ap(c[1]), T.sem[c[4]], T.sem[o["sem"]], pid, rid, topo.mask(core, dst))
+                else:
+                    fold = RemoteDMATransfer(dst_ids=[DstId(rid=rid, pnc=pid)], dma_engine_mask=topo.mask(core, dst), remote_sem=T.sem[c[4]],
+                                             srcs=[ap(c[1]), ap(c[5])], dsts=[ap(c[2])], alu_op=3)
+                    q.remote_dma_fused([fold], local_sem=T.sem[o["sem"]])
             else:
                 emit(q, c).then_inc(T.sem[mark[j][0]], 16 if e == "D" else 1)
-    last = {"sent": sent}
+    last = {}
     for s, v in mark.values():
         last[s] = max(last.get(s, 0), v)
     for s in sorted(last):

import math
import numpy as np
from concourse.bass import DstId, RemoteDMATransfer
from concourse.mybir import AluOpType, ActivationFunctionType

ALU = AluOpType
ACT = ActivationFunctionType
NV, W, I, H = 6, 4096, 256, 128
LN2 = math.log(2.0)
CK = [8192.0 * (4 - d) for d in range(4)]
SPARE = 4160
ZCOL, XW = W, W + SPARE
TINY = -2.0 ** -126
HELD = 64.0
OPT = {"paths": "SSFS", "xc": "S", "pick": "V", "pfs": 1, "turn": 8, "wraph": "V", "wrapc": "V", "nv": "V", "full": "V", "nok": "V", "nokb": "S", "pen": "V",
       "nm": "V", "rsplit": 2, "gsplit": 2, "spare": 2, "b": "V", "wc": "V"}
LEAD, TRIES, SEED, WARM = 8000.0, 3000, 1, 0.006
TIMES = [(0.45, 0.85, 130.0, 2600.0, 50.0, 65.0, 0.5, 1.56), (0.55, 1.05, 180.0, 3300.0, 60.0, 80.0, 0.5, 1.7), (0.65, 1.25, 200.0, 4000.0, 75.0, 100.0, 0.5, 1.9)]
WIDE = {"bfloat16": 2, "float16": 2, "uint16": 2, "float32": 4, "int32": 4}
POOL = {"bfloat16": "pb", "float16": "ph", "uint16": "pu", "float32": "pf", "int32": "pi"}


def build(PE_NS, CYC, LAT, RLAT, VFIX, SFIX, TT2, GR):
    ops, used, slots, hist, tiles, sems = [], {}, {}, {}, [], ["cv", "cs", "ct", "cg"]
    phase, paths = [None, 0], OPT["paths"]

    def view(v, a, b, s=1):
        return {"buf": v["buf"], "lo": v["lo"] + a * v["st"], "n": (b - a + s - 1) // s, "st": v["st"] * s, "dt": v["dt"], "tile": v["tile"], "key": v["key"]}

    def buf(name, n, dt="bfloat16"):
        if name not in slots:
            p = POOL[dt]
            al = 64 // WIDE[dt]
            lo = used.get(p, 0)
            used[p] = lo + (n + al - 1) // al * al
            slots[name] = {"buf": p, "lo": lo, "n": n, "st": 1, "dt": dt, "tile": None, "key": name}
        return slots[name]

    def tile(n=512):
        tiles.append({"acc": [], "bank": None})
        return {"buf": None, "lo": 0, "n": n, "st": 1, "dt": "float32", "tile": len(tiles) - 1, "key": None}

    def span(v):
        return v["lo"], v["lo"] + (v["n"] - 1) * v["st"] + 1

    def add(eng, cost, call, rd, wr, lat=LAT, sem=None, alone=False):
        me = len(ops)
        op = {"eng": eng, "cost": cost, "call": call, "deps": set(), "lat": lat, "sem": sem, "alloc": None, "tiles": set(), "kin": ("", me)}
        if phase[0] is not None and not alone:
            phase[1] += 1
            op["kin"] = tuple(phase)
        for v, w in [(x, False) for x in rd] + [(x, True) for x in wr]:
            if not isinstance(v, dict):
                continue
            if v["tile"] is not None:
                acc = tiles[v["tile"]]["acc"]
                if not acc:
                    op["alloc"] = v["tile"]
                for j, e2, w2 in acc:
                    if j != me and (w or w2 or e2 != eng) and not eng == e2 == "T":
                        op["deps"].add(j)
                    if j != me and eng == e2 == "T":
                        op["after"] = j
                acc.append((me, eng, w))
                op["tiles"].add(v["tile"])
                continue
            lo, hi = span(v)
            lst = hist.setdefault(v["key"], [])
            for j, l2, h2, w2 in lst:
                if j != me and l2 < hi and lo < h2 and (w or w2):
                    op["deps"].add(j)
            if w and v["st"] == 1:
                lst[:] = [x for x in lst if not (lo <= x[1] and x[2] <= hi)]
            lst.append((me, lo, hi, w))
        ops.append(op)
        return me

    def narrow(*vs):
        return all(WIDE[v["dt"]] == 2 and v["tile"] is None for v in vs if isinstance(v, dict))

    def vcost(n, rate):
        return VFIX + max(64.0, n * rate) * CYC

    def TS(out, a, s1, o1, s2=None, o2=None, alone=False):
        add("V", vcost(a["n"], 0.5 if narrow(out, a) else 1.0), ("ts", out, a, s1, s2, o1, o2), [a, s1, s2], [out], alone=alone)
        return out

    def TT(out, a, b, o):
        r = (2.0 if a["tile"] is None and b["tile"] is None else 1.0) * (TT2 if narrow(out, a, b) else 1.0)
        add("V", vcost(a["n"], r), ("tt", out, a, b, o), [a, b], [out])
        return out

    def CP(out, a):
        add("V", vcost(a["n"], 1.0), ("cp", out, a), [a], [out])
        return out

    def SCAN(out, d0, d1, init, o0, o1):
        add("V", vcost(out["n"], 0.5 if narrow(out, d0, d1) else 1.0), ("scan", out, d0, d1, init, o0, o1), [d0, d1], [out])
        return out

    def SET(out, c):
        add("V", vcost(out["n"], 0.5), ("set", out, c), [], [out])
        return out

    def AC(out, a, f, scale=1.0, bias=0.0, acc=None, alone=False):
        add("S", SFIX + max(64.0, a["n"]) * CYC, ("act", out, a, f, scale, bias, acc), [a, scale, bias], [out, acc], alone=alone)
        return out

    def mcost(r):
        return max(64, r["n"]) * PE_NS * (4 if r["dt"] == "float32" else 1) + 5.0

    def MM(groups):
        add("T", sum(mcost(r) for o, ts in groups for l, r in ts), ("mm", groups), [x for o, ts in groups for t2 in ts for x in t2], [o for o, ts in groups])

    def ACC(*parts):
        parts = [p for p in parts if p]
        for k, part in enumerate(parts):
            add("T", sum(mcost(r) for o, l, r in part), ("acc", part, k == 0, k == len(parts) - 1), [x for o, l, r in part for x in (l, r)], [o for o, l, r in part])
        return parts[0][0][0]

    def M1(ts, n=H):
        o = tile(n)
        MM([(o, ts)])
        return o

    def M2(early, late):
        o = tile(H)
        return ACC([(o, l, r) for l, r in early], [(o, l, r) for l, r in late])

    def GATHER(eng, out, win, off, sub=None):
        add(eng, 60.0 + out["n"] * GR * CYC, ("gather", eng, out, win, off, sub), [win, off, sub], [out])
        return out

    def IOTA(out, pat, base, cm):
        add("G", 130.0 + 2 * out["n"] * CYC, ("iota", out, pat, base, cm), [], [out])
        return out

    def DMA(kind, v, name, a, b):
        sem = "d%d" % len(sems)
        sems.append(sem)
        lat = 2000.0 + 128 * v["n"] * WIDE[v["dt"]] / 180.0
        add("D", 60.0, (kind, v, name, a, b, sem), [v] if kind == "store" else [], [v] if kind == "load" else [], lat, sem)

    def SEND(src, dst, hop, cap=None):
        sem = "r%d" % len(sems)
        sems.append(sem)
        lat = RLAT + 128 * src["n"] * WIDE[src["dt"]] / 70.0
        sems.append("s" + sem)
        j = add("G", 400.0, ("send", src, dst, hop, sem, cap), [src, cap], [], 0.0, "s" + sem)
        k = add("R", 0.0, ("recv", hop), [], [dst], lat, sem)
        ops[k]["deps"].add(j)

    X = {"buf": "tab", "lo": 0, "n": XW, "st": 1, "dt": "bfloat16", "tile": None, "key": "tab"}
    ps_in, dv_in, ex_in = buf("ps_in", I), buf("dv_in", I), buf("ex_in", 4 * I)
    nm_in, dn_in = buf("nm_in", I, "int32"), buf("dn_in", 4 * I, "int32")
    wt_in, th_in = buf("wt_in", 1, "int32"), buf("th_in", 1, "int32")
    DMA("load", ps_in, "ps", 0, I)
    DMA("load", view(ex_in, 0, 2 * I), "ex", 0, 2 * I)
    DMA("load", dv_in, "dv", 0, I)
    DMA("load", view(ex_in, 2 * I, 4 * I), "ex", 2 * I, 4 * I)
    for v, name in ((dn_in, "dn"), (nm_in, "nm")):
        DMA("load", v, name, 0, v["n"])
    DMA("load", view(X, 0, W), "xt", 0, W)
    for v, name in ((wt_in, "wt"), (th_in, "th")):
        DMA("load", v, name, 0, 1)
    SET(view(X, W, W + 16), 0.0)

    f32 = lambda name, n=1: buf(name, n, "float32")
    pi_ = IOTA(buf("p_i", 1, "int32"), [[0, 1]], 0, 1)
    mdiff = IOTA(f32("mdiff", 128), [[1, 128]], 0, -1)
    mgrp = IOTA(f32("mgrp", 144), [[16, 9], [0, 16]], 0, 0)
    mvar = IOTA(f32("mvar", 144), [[0, 9], [1, 16]], 0, 0)
    kc = CP(f32("kc"), TS(buf("k_i", 1, "int32"), pi_, 15, ALU.bitwise_and))
    gc = CP(f32("gc"), TS(buf("g_i", 1, "int32"), pi_, 112, ALU.bitwise_and))
    ident = TS(buf("ident", 128), mdiff, 0.0, ALU.is_equal)
    blk = TS(buf("blk", 128), view(mgrp, 0, 128), gc, ALU.is_equal)
    ones = SET(buf("ones", 128), 1.0)
    ones32 = IOTA(f32("ones32", 128), [[0, 128]], 1, 0)
    zeros = SET(buf("zeros", 128), 0.0)
    turn, late = [0], [False]

    def DIAG(out, base, c):
        add("G", 170.0 + 256 * CYC, ("diag", out, base, float(c)), [base], [out], alone=True)
        return out

    def scaled(base, c, name):
        if c == 1.0:
            return base
        if name not in slots:
            turn[0] += 1
            if late[0] and base is ident and not isinstance(c, dict):
                DIAG(buf(name, 128), zeros, c)
            elif turn[0] % OPT["turn"]:
                AC(buf(name, base["n"]), base, ACT.Identity, scale=c, alone=True)
            else:
                TS(buf(name, base["n"]), base, c, ALU.mult, alone=True)
        return slots[name]
    sI = lambda c: scaled(ident, float(c), "I%g" % c)
    sB = lambda c: scaled(blk, float(c), "B%g" % c)
    col = lambda name, a, b: AC(f32(name), kc, ACT.Identity, float(a), float(b))

    def mix(name, i, b):
        return DIAG(buf(name, 128), scaled(blk, b, name + "b") if isinstance(b, dict) else sB(b), i)
    k1, nk1 = col("k1", 1, 1), col("nk1", -1, -1)
    mv = view(mvar, 0, 128)
    IH = mix("IH", 0.5, -0.5)
    tri = TT(buf("c20", 128), TS(buf("c21", 128), mdiff, 0.0, ALU.is_gt, -15.0 / 16, ALU.mult), TS(buf("c22", 128), ident, 17.0 / 16, ALU.mult, -1.0 / 16, ALU.add), ALU.add)
    tri = TT(buf("c23", 128), tri, blk, ALU.mult)
    big = SET(f32("big", 2), 2.0 ** 62)
    Tri = TS(buf("Tri", 128), tri, 2.0 ** 62, ALU.mult, view(big, 0, 1), ALU.mult)
    T2 = TT(buf("T2", 128), TS(buf("c1", 128), mv, 0.0, ALU.is_equal, 8.0, ALU.add), blk, ALU.mult)
    near = TS(buf("c2", 128), AC(f32("c3", 128), mdiff, ACT.Abs), 1.0, ALU.is_equal)
    first8 = TS(f32("first8"), kc, 0.0, ALU.is_equal, -8.0, ALU.mult)
    T1 = TT(buf("T1", 128), TS(buf("c4", 128), TT(buf("c5", 128), near, sI(-2), ALU.add), first8, ALU.add), blk, ALU.mult)
    Z = TT(buf("Z", 144), TS(buf("c6", 144), mgrp, gc, ALU.is_equal), TS(buf("c7", 144), mvar, 15.0, ALU.is_equal), ALU.mult)
    into = lambda z, k: view(z, 15 - k, 143 - k)
    if "V" in OPT["wraph"] + OPT["wrapc"]:
        at = TS(buf("c8", 128), mv, kc, ALU.is_equal, 4.0, ALU.mult)
        Mw = TT(buf("c9", 128), at, TS(buf("c10", 128), mv, k1, ALU.is_equal), ALU.subtract)
        Mw = AC(f32("Mw", 128), Mw, ACT.Identity, 2.0 ** 19)
        n15 = TS(f32("n15"), kc, 15.0, ALU.is_lt)
        fixc = TS(f32("fixc"), n15, 2.0 ** 19, ALU.mult, -32.0, ALU.add)
        fixs = TS(f32("fixs"), n15, -2.0 ** 19, ALU.mult, 65536.0, ALU.add)
    Mkey = IOTA(f32("Mkey", 512), [[0, 128], [1, 4]], 0, 0)
    AC(Mkey, Mkey, ACT.Identity, 2.0 ** 20)
    Lp = mix("Lp", -50, -52)
    Mj, Mf = mix("Mj", -32.5, col("k2h", -0.5, -1)), mix("Mf", -101, col("k2", -1, -2))
    bb = col("bb", 0.5, -106.5)
    Bk16h = scaled(blk, col("k16", 0.5, -8), "Bk16h")
    IHk = [scaled(IH, CK[d] + 4096, "IH%d" % d) for d in range(4)]
    I7k = [mix("I7%d" % d, -6 * CK[d] - 7 * 4096, -7 * CK[d] - 8 * 4096) for d in range(4)]

    def top(out, Wt, acc=None):
        return AC(out, M1([(IH, Wt)]), ACT.Sign, 1.0, TINY, acc)

    def slot(kind, t, h):
        t = t if kind == "i" else t % 2
        sz, sb = buf("%sz%d%d" % (kind, t, h), 4 * H), buf("%sb%d%d" % (kind, t, h), 4 * H)
        sf, so = buf("%sf%d%d" % (kind, t, h), 3 * H, "float16"), buf("%so%d%d" % (kind, t, h), H + 8, "uint16")
        return {"sb": sb, "sf": sf, "so": so, "z": sz, "r": view(sb, 0, H), "un": view(sb, H, 2 * H), "D": view(sb, 2 * H, 3 * H), "q": view(sb, 3 * H, 4 * H), "dn": view(sf, 0, 2 * H),
                "dv": view(sf, 0, H), "nm": view(sf, H, 2 * H), "mc": view(sf, 2 * H, 3 * H), "off": view(so, 0, H), "offc": view(so, H, H + 8)}
    pl = lambda v, d: view(v, d * H, (d + 1) * H)
    nat = lambda v, d: view(v, d, 4 * H, 4)

    dn_own, dn_nxt = buf("dn_own", 8 * H, "float16"), buf("dn_nxt", 8 * H, "float16")
    for h in range(2):
        TS(view(dn_own, 4 * H * h, 4 * H * (h + 1)), view(dn_in, 4 * H * h, 4 * H * (h + 1)), -2048.0, ALU.add)
    SEND(dn_own, dn_nxt, -1)

    def logic(t, h, r, r2, z, a, pf, full, oc, S, dnc):
        b = lambda name, n=H, dt="bfloat16": buf("L%s%d%d" % (name, t % 2, h), n, dt)
        phase[:] = ["L%d%d" % (h, t > 0), 0]
        tt = b("t", 4 * H)
        if OPT["pick"] == "V":
            for d in range(4):
                TT(pl(tt, d), pl(z, d), pf, ALU.mult)
        elif OPT["pick"] == "P":
            PK = tile()
            MM([(pl(PK, d), [(ident, pf)]) for d in range(4)])
            TT(tt, PK, z, ALU.mult)
        else:
            PK = tile()
            ACC([(PK, ident, z)], [(pl(PK, d), sI(128), pf) for d in range(4)])
            AC(tt, PK, ACT.Relu, 1.0, -128.0)
        R = b("R", 4 * H)
        for j in range(OPT["rsplit"]):
            w = 4 * H // OPT["rsplit"]
            AC(view(R, w * j, w * (j + 1)), M1([(blk, view(tt, w * j, w * (j + 1)))], w), ACT.Relu, 1.0, nk1)
        G = M2([(T2, pl(tt, d)) for d in range(4)] + [(sB(-64), full)] + ([(Boc, oc)] if oc else []), [(T1, pl(R, d)) for d in range(4)])
        g1 = AC(b("g1"), G, ACT.Relu, -1.0, -31.5 if oc else 33.0)
        Wm = AC(b("Wm"), M2([(ident, r)], [(sI(-512), g1)]), ACT.Exp, LN2, -117 * LN2)
        cnt = f32("cnt%d%d" % (t, h)) if t < NV - 1 else None
        jf = top(b("jf"), Wm, cnt)
        none = TS(b("none"), M1([(sI(-64), pf), (blk, g1)]), -48.0, ALU.is_equal)
        q = AC(S["q"], M1([(ident, pf), (IH, jf)]), ACT.Relu, 0.5, -3.5)
        KP = tile()
        early = [(KP, ident, dnc)] + [(nat(KP, d), sI(-65536), pl(a, d)) for d in range(4)] + [(nat(KP, 0), sI(6553600), full)]
        ACC(early + [(nat(KP, d), I7k[d], pf) for d in range(4)], [(nat(KP, 0), sI(17 * 65536), none)] + [(nat(KP, d), IHk[d], jf) for d in range(4)])
        m = nat(SCAN(tile(), Mkey, KP, 0.0, ALU.min, ALU.max), 3)
        late[0] = True
        rnd = 1.5 * 2.0 ** 36
        TS(S["D"], m, rnd, ALU.add, -rnd, ALU.add)
        TT(S["mc"], m, S["D"], ALU.subtract)
        RR = tile(2 * H)
        MM([(pl(RR, 0), [(sB(95), pf), (sI(-320), full), (sI(-161), jf)]), (pl(RR, 1), [(Lp, pf), (blk, jf)])])
        TT(S["r"], pl(RR, 1), TT(b("r1"), pl(RR, 0), r2, ALU.min), ALU.max)
        TS(S["un"], S["r"], 0.0, ALU.is_lt)
        cP = M2([(sB(2080), pf)], [(blk, S["mc"])])
        LP = M2([(sB(208896), pf), (sI(2 ** 23), S["un"])], [(sB(101), S["mc"])])
        e = TT(b("e", H, "int32"), cP, S["nm"], ALU.mult)
        TS(e, e, 5, ALU.arith_shift_right, 4095, ALU.bitwise_and)
        TT(e, LP, e, ALU.add)
        TS(e, e, 0x800FFF, ALU.bitwise_and)
        TS(S["off"], e, float(ZCOL), ALU.min)
        if OPT["wrapc"] == "V":
            sc = SCAN(b("sc", H, "float32"), Mw, cP, 0.0, ALU.add, ALU.min)
            TS(S["offc"], view(sc, 15, H, 16), fixc, ALU.add)
        else:
            TS(S["offc"], M1([(into(Z, k), view(S["mc"], k, H, 16)) for k in range(16)], 8), 2048.0, ALU.add)
        if t > 0:
            for k in ("so", "sb", "sf"):
                SEND(S[k], slot("i", t, h)[k], 1)
        W2 = AC(b("W2"), M1([(ident, r), (sI(-512), g1), (sI(-256), jf)]), ACT.Exp, LN2, -373 * LN2)
        j2 = top(b("j2"), W2)
        x = AC(b("x"), M1([(sI(16), jf), (Bk16h, j2)]), ACT.Relu, 1.0, -67.0)
        DF = tile()
        if OPT["b"] == "V":
            sh = TS(b("b", H, "float16"), M1([(Mj, jf), (Mf, full), (sI(-18), none), (sI(1 / 32), x)]), bb, ALU.add)
            ACC([(DF, ident, a)], [(pl(DF, d), ident, sh) for d in range(4)])
        else:
            sh = AC(b("b"), M1([(Mj, jf), (Mf, full), (sI(-18), none)]), ACT.Identity, 1.0, bb)
            ACC([(DF, ident, a)] + [(pl(DF, d), ident, sh) for d in range(4)], [(pl(DF, d), sI(1 / 32), x) for d in range(4)])
        if t > 0:
            SEND(a, slot("i", t, h)["z"], 1, AC(S["z"], DF, ACT.Abs, 32.0))
        else:
            TT(S["z"], AC(DF, DF, ACT.Abs, 32.0), a, ALU.min)
        if t < NV - 1 and h == 1:
            n = TS(buf("cn%d" % t, 1, "int32"), M1([(ones32, f32("cnt%d0" % t)), (ones32, cnt)], 1), 0.5, ALU.mult, 16384.0, ALU.add)
            TS(n, n, 7, ALU.bitwise_and)
            SEND(TS(f32("ao%d" % t), n, -32.0, ALU.mult), f32("ai%d" % (t + 1)), 2 if t > 0 else 1)

    def reads(t, h, S, thA):
        b = lambda name, n=H, dt="bfloat16": buf("G%s%d" % (name, h), n, dt)
        phase[:] = ["G%d" % h, 0]
        win = view(X, 0, W + 16)
        fused = "F" in paths[2 * h:2 * h + 2]
        xc = view(seeds[h], 0, 2048, 16) if fused else b("xc")
        GATHER(OPT["xc"], xc, win, S["offc"])
        SP, y, ad, ym = tile(H), b("y", 2048), b("ad", 2048), b("ym", 2048)
        for c in range(2):
            path = paths[2 * h + c]
            yc, ac, xcc, off = view(y, 1024 * c, 1024 * (c + 1)), view(ad, 1024 * c, 1024 * (c + 1)), view(xc, 64 * c, 64 * (c + 1)), view(S["off"], 64 * c, 64 * (c + 1))
            gs = OPT["gsplit"]
            n = 1024 // gs
            part = lambda v, j, w: view(v, w * j, w * (j + 1))
            if path == "F":
                rep = SCAN(buf("rep%d%d" % (h, c), 1024), Mrun, view(seeds[h], 1024 * c, 1024 * (c + 1)), 0.0, ALU.min, ALU.max)
                for j in range(gs):
                    GATHER("V", part(yc, j, n), win, part(off, j, n // 16), part(rep, j, n))
                    AC(part(ac, j, n), part(yc, j, n), ACT.Abs)
                lanes = [view(ac, k, 1024, 16) for k in range(16)]
            else:
                for j in range(gs):
                    GATHER(path, part(yc, j, n), win, part(off, j, n // 16))
                for half in range(2):
                    DP = tile()
                    MM([(part(DP, j, 64), [(ident, view(yc, 8 * half + j, 1024, 16)), (sI(-1), xcc)]) for j in range(8)])
                    AC(part(ac, half, 512), DP, ACT.Abs)
                lanes = [part(ac, k, 64) for k in range(16)]
            MM([(part(SP, c, 64), [(sI(8192), part(S["un"], c, 64))] + [(into(Z, k), lanes[k]) for k in range(16)])])
            SCAN(part(ym, c, 1024), Mrun, yc, 0.0, ALU.min, ALU.max)
        if OPT["wc"] == "V":
            cf = TS(b("cf"), SP, thA, ALU.add, 0.0, ALU.is_le)
        else:
            cf = AC(b("cf"), AC(SP, SP, ACT.Sign, -1.0, thA), ACT.Relu)
        return xc, view(ym, 15, 2048, 16), cf

    def update(t, h, S, got, N_):
        xc, Y, cf = got
        b = lambda name, n=H, dt="bfloat16": buf("U%s%d%d" % (name, t % 2, h), n, dt)
        last = t == NV - 1
        phase[:] = ["U%d%d" % (h, last), 0]
        r, un, q, z = S["r"], S["un"], S["q"], S["z"]
        npv = AC(b("np"), M1([(ident, r), (sI(256), top(b("ny"), AC(b("Wy"), r, ACT.Exp, LN2, -117 * LN2)))]), ACT.Relu, 1.0, -255.0)
        pen = b("pen", 4 * H)
        c0, c1 = (67.0 / 32, -32) if last else (95.0 / 32, -128)
        for d in range(4):
            TS(pl(pen, d), S["D"], CK[d], ALU.not_equal, -c0 if last else c0, ALU.add)
        hn = TT(b("hn"), q, S["D"], ALU.is_gt)
        Wo = AC(b("Wo"), M1([(ident, r), (sI(512), un), (sB(512), hn)]), ACT.Exp, -LN2, 120 * LN2)
        oc = top(b("oc"), TT(b("Wc"), Wo, cf, ALU.mult))
        cnt = M2([(blk, hn)], [(blk, cf)])
        nokb = AC(b("nokb"), cnt, ACT.Sign) if OPT["nokb"] == "S" else TS(b("nokb"), cnt, 0.5, ALU.is_gt)
        pf = full = None
        if not last:
            pA = AC(b("pA"), M1([(Tri, un), (Tq, q), (IH, Wo)]), ACT.Sign, 1.0, TINY)
            if OPT["pfs"]:
                pf = TT(b("pf"), nokb, AC(b("s"), M1([(sI(-2), q), (sI(-1), pA)]), ACT.Identity, 1.0, 1.0), ALU.is_equal)
            else:
                pf = TS(b("pf"), M2([(sI(2), q), (ident, pA)], [(ident, nokb)]), 1.0, ALU.is_equal)
            full = TT(b("full"), pf, un, ALU.is_gt) if OPT["full"] == "V" else AC(b("full"), M2([(sI(-1), un)], [(ident, pf)]), ACT.Relu)
        if OPT["nok"] == "V":
            nok = TT(b("nok"), nokb, q, ALU.is_ge)
        else:
            nok = AC(b("nok"), M2([(sI(-2), q)], [(ident, nokb)]), ACT.Identity, 1.0, 1.0)
        r2 = TT(b("r"), M2([(blk, npv)], [(sI(-512), nok)]), r, ALU.max)
        U5 = tile()
        if last:
            er = TS(b("er"), M1([(ident, S["dv"]), (sI(32), un)]), 0.0, ALU.is_gt)
            zs = view(zs_in, H * h, H * (h + 1))
            bit = TT(b("bx", H, "float32"), M1([(Bpow, er), (sB(2), q)]), AC(b("pw"), zs, ACT.Exp, -LN2), ALU.mult)
            bit = TS(b("bit", H, "int32"), bit, -0.5, ALU.add)
            gone = TT(b("gone"), TS(bit, bit, 1, ALU.bitwise_and), er, ALU.add)
            zf = TS(b("zf"), M1([(ident, zs), (sI(-32), gone)]), 0.0, ALU.max, 128.0, ALU.add)
            ZR = tile()
            ACC([(ZR, sI(-2), z)], [(pl(ZR, d), ident, zf) for d in range(4)])
            zr = TT(b("zr", 4 * H), ZR, z, ALU.min)
            zb = AC(b("zb", 4 * H), zr, ACT.Relu, 18.0, -288.0)
            ZP = tile()
            MM([(nat(ZP, d), [(ident, pl(zr, d)), (sI(-1), pl(zb, d))]) for d in range(4)])
            exr = AC(b("exr", 4 * H), ZP, ACT.Identity, 1.0, -1.0)
            MM([(nat(U5, d), [(sI(c1), pl(pen, d)), (Bkh, oc)]) for d in range(4)])
            a = TT(view(yg, 4 * H * h, 4 * H * (h + 1)), U5, exr, ALU.max)
            TT(S["dv"], TS(b("dw", H, "float16"), S["dv"], 0.0, ALU.is_lt, 16.0, ALU.mult), S["dv"], ALU.add)
        else:
            ACC([(U5, sI(c1), pen)], [(pl(U5, d), Bv, oc) for d in range(4)], [(pl(U5, d), sI(164), full) for d in range(4)])
            a = TT(b("a", 4 * H), U5, z, ALU.max)
        if OPT["nm"] == "V":
            CLP = tile()
            MM([(pl(CLP, 0), [(sI(1 / 8192), S["D"]), (sI(-32), nok)]), (pl(CLP, 1), [(ident, S["mc"]), (sI(-8192), nok)]),
                (pl(CLP, 2), [(sI(1 / 8192), S["D"]), (sI(32), nok)]), (pl(CLP, 3), [(ident, S["mc"]), (sI(8192), nok)])])
            TT(N_["dn"], view(CLP, 2 * H, 4 * H), TT(b("n1", 2 * H, "float16"), view(CLP, 0, 2 * H), S["dn"], ALU.max), ALU.min)
        else:
            df, CLP = b("df", 2 * H, "float16"), tile(2 * H)
            MM([(pl(CLP, 0), [(sI(1 / 8192), S["D"]), (sI(-1), S["dv"])]), (pl(CLP, 1), [(ident, S["mc"]), (sI(-1), S["nm"])])])
        HV = tile(2 * H)
        groups = []
        for c in range(2):
            s = lambda v: view(v, 64 * c, 64 * (c + 1))
            f = paths[2 * h + c] == "F"
            groups.append((s(pl(HV, 1)), [(sI(-0.25), s(ones)), (sI(1 if f else 0.5), s(xc)), (sI(0.5), s(Y))]))
            if OPT["wraph"] == "V":
                groups.append((s(pl(HV, 0)), ([(Wb, s(xc))] if f else []) + [(Wb, s(Y))] + ([(sI(65536), s(nokb))] if OPT["spare"] == 2 else [])))
            else:
                groups.append((view(HV, 4 * c, 4 * c + 4), [(into(Zw, k), view(s(v), k, 64, 16)) for k in range(16) for v in ([xc, Y] if f else [Y])]))
        MM(groups)
        sh = view(SCAN(b("sh", H, "float32"), Mw, pl(HV, 0), 0.0, ALU.add, ALU.min), 15, H, 16) if OPT["wraph"] == "V" else view(HV, 0, 8)
        rnd = 1.5 * 2.0 ** 23
        if OPT["nv"] == "V":
            nv = TS(b("nv"), pl(HV, 1), rnd, ALU.add, -rnd, ALU.add)
        else:
            nv = AC(b("nv"), AC(b("nw", H, "float32"), pl(HV, 1), ACT.Identity, 1.0, rnd), ACT.Identity, 1.0, -rnd)
        hi = CP(b("hi", 8, "int32"), sh)
        TS(hi, hi, 15, ALU.bitwise_and)
        if OPT["spare"] == 2:
            base = TT(b("base", 8, "float32"), TS(b("fl", 8, "float32"), sh, fixs, ALU.is_ge, float(SPARE), ALU.mult), view(c16, 0, 8), ALU.add)
            offs = CP(b("so", 8, "uint16"), TT(hi, base, hi, ALU.add))
            win = view(X, W // 2 * h, W // 2 * (h + 1) + SPARE)
        elif OPT["spare"]:
            base = tile(8)
            ACC([(base, ident, c16h)], [(base, into(Zs, k), view(nokb, k, H, 16)) for k in range(16)])
            offs = CP(b("so", 8, "uint16"), TT(hi, base, hi, ALU.add))
            win = view(X, W // 2 * h, W // 2 * (h + 1) + SPARE)
        else:
            offs = CP(b("so", 8, "uint16"), TT(hi, view(c16, 0, 8), hi, ALU.add))
            win = view(X, W // 2 * h, W // 2 * (h + 1))
            val = GATHER(OPT["xc"], b("old"), win, offs)
            for sign, o in ((-1, ALU.max), (1, ALU.min)):
                val = TT(b("val%d" % sign), M2([(ident, nv)], [(sI(256 * sign), nokb)]), val, o)
            nv = val
        add("V", 60.0 + H * 3.8 * CYC, ("scatter", win, offs, nv), [offs, nv], [win])
        return r2, a, pf, full, oc

    zs_own, zs_in = buf("zs_own", I), buf("zs_in", I)
    for h in range(2):
        S = slot("i", 0, h)
        b = lambda name, n=H, dt="bfloat16": buf("P%s%d" % (name, h), n, dt)
        p, dv = view(ps_in, H * h, H * (h + 1)), view(dv_in, H * h, H * (h + 1))
        r0 = TT(b("r0"), TS(b("r00"), p, 64.0, ALU.mult), p, ALU.min)
        un = TS(b("un"), p, 0.0, ALU.is_lt)
        Wo = AC(b("Wo"), M1([(ident, p), (sI(512), un)]), ACT.Exp, -LN2, 120 * LN2)
        pf = TS(b("pf"), M1([(Tri, un), (IH, Wo)]), 0.0, ALU.is_gt)
        full = TT(b("full"), pf, un, ALU.is_gt)
        e = view(ex_in, 4 * H * h, 4 * H * (h + 1))
        zb = AC(b("zb", 4 * H), e, ACT.Relu, -18.0, -18.0)
        ZP = tile()
        MM([(pl(ZP, d), [(ident, nat(e, d)), (ident, nat(zb, d))]) for d in range(4)])
        z0 = AC(b("z0", 4 * H), ZP, ACT.Identity, 1.0, 1.0)
        x, held = TT(b("x"), TS(b("x0"), un, 8.0, ALU.mult), dv, ALU.add), b("held", 4 * H)
        for d in range(4):
            TS(pl(held, d), x, float(d), ALU.is_equal, HELD, ALU.mult)
        FP = tile()
        ACC([(FP, ident, held)], [(pl(FP, d), sI(100), full) for d in range(4)])
        a = TT(b("a", 4 * H), TS(FP, FP, 100.0, ALU.min), z0, ALU.max)
        TS(S["dv"], dv, -1.0, ALU.mult, -12.0, ALU.add)
        TS(S["nm"], view(nm_in, H * h, H * (h + 1)), -2048.0, ALU.add)
        logic(0, h, r0, r0, z0, a, pf, full, None, S, view(dn_own, 4 * H * h, 4 * H * (h + 1)))
        phase[0] = None
        zx = TT(held, held, z0, ALU.min)
        AC(view(zs_own, H * h, H * (h + 1)), M1([(ident, pl(zx, d)) for d in range(4)]), ACT.Identity)
    SEND(zs_own, zs_in, NV - 1)

    Tq = scaled(Tri, -2.0, "Tq")
    Boc = mix("Boc", 4.5, 4)
    Bv, Bkh = scaled(blk, col("k63", 0.5, -31.5), "Bv"), scaled(blk, col("k1h", 0.5, 0.5), "Bkh")
    Bpow = scaled(blk, CP(f32("pw2"), AC(buf("pw1", 1), k1, ACT.Exp, LN2)), "Bpow")
    wt = CP(f32("wt"), wt_in)
    Wb, Zw = (scaled(blk, wt, "Wb"), None) if OPT["wraph"] == "V" else (None, scaled(Z, wt, "Zw"))
    c16 = TS(f32("c16", 16), IOTA(f32("c11", 16), [[16, 16]], 0, 0), kc, ALU.add, 16.0, ALU.mult)
    if OPT["spare"] == 1:
        Zs, c16h = scaled(Z, SPARE / 16.0, "Zs"), CP(buf("c16h", 8, "float16"), view(c16, 0, 8))
    Mrun = IOTA(buf("Mrun", 1024), [[0, 64], [2048, 16]], -1024, 0)
    seeds = [buf("seed%d" % h, 2048) for h in range(2)]
    for c in range(4):
        if paths[c] == "F":
            IOTA(view(seeds[c // 2], 1024 * (c % 2), 1024 * (c % 2 + 1)), [[0, 1024]], 0, 0)
    nth = TS(f32("nth"), th_in, -1.0, ALU.mult)

    yn, yp, yd, yg = f32("yn_s", I), buf("yp_s", I), buf("yd_s", I), buf("yg_s", 4 * I)
    for t in range(NV):
        phase[:] = ["A", 0]
        thA = nth if t == 0 else TS(f32("thA%d" % t), f32("ai%d" % t), nth, ALU.add)
        got = [reads(t, h, slot("i", t, h), thA) for h in range(2)]
        for h in range(2):
            N_, S = slot("o", t + 1, h), slot("i", t, h)
            r2, a, pf, full, oc = update(t, h, S, got[h], N_)
            if t < NV - 1:
                logic(t + 1, h, S["r"], r2, S["z"], a, pf, full, oc, N_, view(dn_nxt, 4 * H * h, 4 * H * (h + 1)))
            else:
                phase[0] = None
                s = lambda v: view(v, H * h, H * (h + 1))
                DMA("store", view(X, W // 2 * h, W // 2 * (h + 1)), "yx", W // 2 * h, W // 2 * (h + 1))
                TS(s(yn), N_["nm"], 2048.0, ALU.add)
                TS(s(yd), N_["dv"], -1.0, ALU.mult, 4.0, ALU.add)
                TT(s(yp), TS(buf("o1%d" % h, H), r2, -1.0, ALU.max), AC(buf("o2%d" % h, H), r2, ACT.Identity, 1.0, 64.0), ALU.min)
                DMA("store", a, "yg", 4 * H * h, 4 * H * (h + 1))
                ops[-1]["tail"] = LEAD * (1 - h)
    for v, name in ((yn, "yn"), (yp, "yp"), (yd, "yd")):
        DMA("store", v, name, 0, I)
    return ops, tiles, used, sems


def schedule(ops, tiles, costs):
    n = len(ops)
    eng, alloc = [o["eng"] for o in ops], [o["alloc"] for o in ops]
    pred = [sorted(o["deps"] | ({o["after"]} if "after" in o else set())) for o in ops]
    succ = [[] for _ in ops]
    for j in range(n):
        for d in pred[j]:
            succ[d].append(j)
    users = [sorted({a[0] for a in t["acc"]}) for t in tiles]
    cost, lat = costs[0]
    kin = [o["kin"] for o in ops]

    def run(off):
        prio = [0.0] * n
        for j in range(n - 1, -1, -1):
            prio[j] = cost[j] + lat[j] + off.get(kin[j], 0.0) + max([prio[s] for s in succ[j]] + [ops[j].get("tail", 0.0)])
        left, ready = [len(p) for p in pred], [0.0] * n
        pool = {e: [j for j in range(n) if not left[j] and eng[j] == e] for e in "VSTGDR"}
        free = {e: 0.0 for e in pool}
        todo, end, bank, seq, took = [len(u) for u in users], [0.0] * len(tiles), [None] * 8, [], {}
        for _ in range(n):
            room = min([(0.0 if bank[k] is None else end[bank[k]], k) for k in range(8) if bank[k] is None or todo[bank[k]] == 0], default=None)
            best = None
            for e, p in pool.items():
                f = free[e]
                for j in p:
                    at = ready[j] if ready[j] > f else f
                    if alloc[j] is not None:
                        if room is None:
                            continue
                        at = max(at, room[0])
                    if best is None or (at, -prio[j], j) < best:
                        best = (at, -prio[j], j)
            if best is None:
                return None
            at, _, j = best
            e = eng[j]
            lim, most = at + 0.3 * cost[j], prio[j] + 500.0
            for i in pool[e]:
                if ready[i] < lim and prio[i] > most and (alloc[i] is None or (room is not None and room[0] < lim)):
                    j, most = i, prio[i]
                    at = max(ready[i], free[e], room[0] if alloc[i] is not None else 0.0)
            if alloc[j] is not None:
                took[j] = (room[1], bank[room[1]])
                bank[room[1]] = alloc[j]
            pool[e].remove(j)
            seq.append(j)
            if e != "R":
                free[e] = at + cost[j]
            fin = at + cost[j] + lat[j]
            for tl in ops[j]["tiles"]:
                todo[tl] -= 1
                end[tl] = max(end[tl], fin)
            for s in succ[j]:
                ready[s] = max(ready[s], fin)
                left[s] -= 1
                if left[s] == 0:
                    pool[eng[s]].append(s)
        return seq, took

    def length(seq, took, c, l):
        fin, free = [0.0] * n, {e: 0.0 for e in "VSTGDR"}
        for j in seq:
            at = max([free[eng[j]]] + [fin[d] for d in pred[j]])
            if j in took and took[j][1] is not None:
                at = max([at] + [fin[d] for d in users[took[j][1]]])
            if eng[j] != "R":
                free[eng[j]] = at + c[j]
            fin[j] = at + c[j] + l[j]
        return fin

    kinds = sorted(set(kin))
    rng = np.random.default_rng(SEED)
    off, plan = {}, run({})
    while plan is None:
        off = {k: float(rng.normal()) * 300.0 for k in kinds}
        plan = run(off)
    base = [max(length(plan[0], plan[1], c, l)) for c, l in costs]
    best = float(len(costs))
    now = best
    for it in range(TRIES):
        o2 = dict(off)
        for _ in range(2 ** int(rng.integers(0, 3))):
            k = kinds[int(rng.integers(0, len(kinds)))]
            o2[k] = o2.get(k, 0.0) + float(rng.normal()) * (300.0, 1000.0, 3000.0)[int(rng.integers(0, 3))]
        p2 = run(o2)
        if p2 is not None:
            v = sum(max(length(p2[0], p2[1], c, l)) / b for (c, l), b in zip(costs, base))
            if v <= now + WARM * (1 - it / TRIES) * float(rng.random()):
                now, off = v, o2
            if v < best:
                best, plan = v, p2
    seq, took = plan
    for j, (k, old) in took.items():
        tiles[alloc[j]]["bank"] = k
        if old is not None:
            ops[j]["deps"] |= set(users[old])
    return {e: [j for j in seq if eng[j] == e] for e in "VSTGDR"}, [length(seq, took, c, l) for c, l in costs]


OPS, TILES, USED, SEMAPHORES = build(*TIMES[0])
ORDER, ENDS = schedule(OPS, TILES, [([o["cost"] for o in p], [o["lat"] for o in p]) for p in [build(*t)[0] for t in TIMES]])
SCRATCH = {"tab": ("sbuf", [128, XW], "bfloat16")}
SCRATCH.update({p: ("sbuf", [128, USED[p]], d) for d, p in POOL.items()})
SCRATCH.update({"bank%d" % k: ("psum", [128, 512], "float32") for k in range(8)})


def rank_program(g, core, T, topo):
    rank = T.rank_of(core)
    if rank is None:
        return
    cores = T.cores
    queue = {"V": g.vector, "S": g.scalar, "T": g.tensor, "G": g, "D": g.sync}
    counter = {"V": "cv", "S": "cs", "T": "ct", "G": "cg"}

    def ap(v):
        if not isinstance(v, dict):
            return v
        t = T[v["buf"]] if v["tile"] is None else T["bank%d" % TILES[v["tile"]]["bank"]]
        if v["st"] == 1:
            return t[:, v["lo"]:v["lo"] + v["n"]]
        return t[:, v["lo"]:v["lo"] + (v["n"] - 1) * v["st"] + 1:v["st"]]

    mark = {}
    for e in ORDER:
        k = 0
        for j in ORDER[e]:
            o = OPS[j]
            if e == "R":
                mark[j] = (o["sem"], len(topo.engines(cores[(rank - o["call"][1]) % len(cores)], core)))
            elif e == "D":
                mark[j] = (o["sem"], 16)
            elif o["sem"] is None:
                k += 1
                mark[j] = (counter[e], k)
            else:
                mark[j] = (o["sem"], len(topo.engines(core, cores[(rank + o["call"][3]) % len(cores)])))

    def emit(q, c):
        kind = c[0]
        if kind == "ts":
            if c[6] is None:
                return q.tensor_scalar(ap(c[1]), ap(c[2]), ap(c[3]), None, c[5])
            return q.tensor_scalar(ap(c[1]), ap(c[2]), ap(c[3]), ap(c[4]), c[5], c[6])
        if kind == "tt":
            return q.tensor_tensor(ap(c[1]), ap(c[2]), ap(c[3]), c[4])
        if kind == "cp":
            return q.tensor_copy(ap(c[1]), ap(c[2]))
        if kind == "scan":
            return q.tensor_tensor_scan(ap(c[1]), ap(c[2]), ap(c[3]), c[4], c[5], c[6])
        if kind == "set":
            return q.memset(ap(c[1]), c[2])
        if kind == "act":
            if c[6] is not None:
                return q.activation(ap(c[1]), ap(c[2]), c[3], bias=c[5], scale=c[4], accum_out=ap(c[6]))
            return q.activation(ap(c[1]), ap(c[2]), c[3], bias=ap(c[5]), scale=ap(c[4]))
        if kind == "mm":
            for out, ts in c[1]:
                for k, (l, r) in enumerate(ts):
                    last = q.matmul(ap(out), ap(l), ap(r), k == 0, k == len(ts) - 1)
            return last
        if kind == "acc":
            for k, (out, l, r) in enumerate(c[1]):
                last = q.matmul(ap(out), ap(l), ap(r), c[2] and k == 0, c[3] and k == len(c[1]) - 1)
            return last
        if kind == "gather":
            src = ap(c[3]).indirect(ap(c[4]))
            if c[5] is not None:
                return q.tensor_tensor(ap(c[2]), src, ap(c[5]), ALU.subtract)
            return q.tensor_copy(ap(c[2]), src) if c[1] == "V" else q.activation(ap(c[2]), src, ACT.Copy)
        if kind == "scatter":
            return q.tensor_copy(ap(c[1]).indirect(ap(c[2])), ap(c[3]))
        if kind == "diag":
            return q.affine_select(ap(c[1]), ap(c[2]), [[-1, 128]], ALU.not_equal, c[3], 0, 1)
        if kind == "iota":
            if c[1]["dt"] == "int32":
                return q.iota(ap(c[1]), c[2], c[3], c[4])
            return q.iota(ap(c[1]), c[2], c[3], c[4], allow_small_or_imprecise_dtypes=True)
        whole = T[c[2]].shape[1] == c[4] - c[3]
        side = T[c[2]][:] if whole else T[c[2]][:, c[3]:c[4]]
        return q.dma_start(ap(c[1]), side) if kind == "load" else q.dma_start(side, ap(c[1]))

    for e, q in queue.items():
        seen = {}
        for j in ORDER[e]:
            o = OPS[j]
            need = {}
            for d in o["deps"]:
                s, v = mark[d]
                need[s] = max(need.get(s, 0), v)
            c = o["call"]
            for s in sorted(need):
                if need[s] > seen.get(s, 0):
                    q.wait_ge(T.sem[s], need[s])
                    seen[s] = need[s]
            if c[0] == "send":
                dst = cores[(rank + c[3]) % len(cores)]
                rid, pid, _ = topo.addr(dst)
                if c[5] is None:
                    q.remote_dma(ap(c[2]), ap(c[1]), T.sem[c[4]], T.sem[o["sem"]], pid, rid, topo.mask(core, dst))
                else:
                    fold = RemoteDMATransfer(dst_ids=[DstId(rid=rid, pnc=pid)], dma_engine_mask=topo.mask(core, dst), remote_sem=T.sem[c[4]],
                                             srcs=[ap(c[1]), ap(c[5])], dsts=[ap(c[2])], alu_op=3)
                    q.remote_dma_fused([fold], local_sem=T.sem[o["sem"]])
            else:
                emit(q, c).then_inc(T.sem[mark[j][0]], 16 if e == "D" else 1)
    last = {}
    for s, v in mark.values():
        last[s] = max(last.get(s, 0), v)
    for s in sorted(last):
        g.wait_ge(T.sem[s], last[s])
